import numpy as np
import ml_dtypes


def mxq(x, axis, fmt="e4m3"):
    dtype, down = {"e4m3": (ml_dtypes.float8_e4m3fn, 7), "e5m2": (ml_dtypes.float8_e5m2, 14)}[fmt]
    v = np.moveaxis(np.asarray(x, np.float32).astype(ml_dtypes.bfloat16).astype(np.float64), axis, -1)
    blocks = v.reshape(v.shape[:-1] + (-1, 32))
    amax = np.abs(blocks).max(-1, keepdims=True)
    byte = np.maximum(np.where(amax > 0, np.frexp(amax)[1] - 1 + 127, 0) - down, 1)
    scale = np.exp2(byte - 127.0)
    codes = (blocks / scale).astype(np.float32).astype(dtype).astype(np.float64)
    return np.moveaxis((codes * scale).reshape(v.shape), -1, axis)


WIDE = False


def mx_kscale(k):
    if not WIDE:
        return np.ones(k)
    levels = np.array([10, -10, 5, -5, 0])
    if k % 512:
        return np.exp2(np.random.permutation(np.resize(levels, k // 32))).repeat(32)
    a = np.empty((k // 512, 16))
    for p in range(k // 512):
        a[p, :8] = np.random.permutation(np.resize(levels, 8))
        for g in range(8):
            far = levels[np.abs(levels - a[p, g]) >= 10]
            a[p, g + 8] = far[np.random.randint(len(far))]
    return np.exp2(a.ravel()).repeat(32)


def f64(x):
    return np.asarray(x).astype(np.float64)


def striped(idx):
    return np.tile(np.asarray(idx).reshape(-1, 16).T, (8, 1)).astype(np.uint16)


def unstriped(offs):
    return offs[:16].T.reshape(-1).astype(np.int64)


E2M1 = np.array([0.0, 0.5, 1.0, 1.5, 2.0, 3.0, 4.0, 6.0, -0.0, -0.5, -1.0, -1.5, -2.0, -3.0, -4.0, -6.0])


def pack_weight(w, fmt):
    k, n = w.shape
    w = f64(np.asarray(w, np.float32).astype(ml_dtypes.bfloat16)).reshape(k // 32, 32, n)
    amax = np.abs(w).max(1)
    if fmt == "e4m3":
        byte = np.frexp(amax)[1] - 1 + 127 - 7
    else:
        mant, ex = np.frexp(amax / 6.0)
        byte = np.where(mant > 0.5, ex, ex - 1) + 127
    byte = np.clip(np.where(amax > 0, byte, 1), 1, 254)
    scaled = (w * np.exp2(127.0 - byte)[:, None, :]).reshape(k, n).astype(np.float32)
    by_word = np.ascontiguousarray(scaled.reshape(k // 512, 128, 4, n).transpose(0, 1, 3, 2))
    if fmt == "e4m3":
        words = by_word.astype(ml_dtypes.float8_e4m3fn).view(np.uint8)
    else:
        c = by_word.astype(ml_dtypes.float4_e2m1fn).view(np.uint8) & 0xF
        words = (c[..., 0::2] | (c[..., 1::2] << 4)).reshape(k // 512, 128, 2 * n)
    return np.ascontiguousarray(words), np.ascontiguousarray(byte.astype(np.uint8).reshape(k // 512, 16, n))


def unpack_weight(words, scales, fmt):
    g, _, n = scales.shape
    words = np.ascontiguousarray(words).reshape(g, 128, n, -1)
    if fmt == "e4m3":
        vals = words.view(ml_dtypes.float8_e4m3fn).astype(np.float64)
    else:
        nib = np.empty((g, 128, n, 4), np.uint8)
        nib[..., 0::2] = words & 0xF
        nib[..., 1::2] = words >> 4
        vals = E2M1[nib]
    vals = vals * np.repeat(np.exp2(scales.astype(np.float64) - 127.0), 8, axis=1)[..., None]
    return vals.transpose(0, 1, 3, 2).reshape(g * 512, n)


D, E, T, I, Q, G = 512, 512, 2048, 512, 128, 64


def setup_inputs():
    n = np.random.standard_normal
    idx = np.random.permutation(T)[:I]
    fd = mx_kscale(D)
    fe = mx_kscale(E)
    keysp = pack_weight(n((D, T)) / fd[:, None], "e2m1")
    valsp = pack_weight(n((E, T)) / fe[:, None], "e2m1")
    return {
        "query": (n((D, Q)) * 0.5 / np.sqrt(D) * fd[:, None]).astype(np.float32),
        "keys_words": keysp[0],
        "keys_scales": keysp[1],
        "gout": (n((E, Q)) * 1 / np.sqrt(E) * fe[:, None]).astype(np.float32),
        "vals_words": valsp[0],
        "vals_scales": valsp[1],
        "size": (np.random.uniform(0.5, 2.0, (1, I))).astype(np.float32),
        "dquery": (n((D, Q)) * 1.0 / np.sqrt(D) * fd[:, None]).astype(np.float32),
        "base": (0.5 * n((Q, I))).astype(np.float32),
        "offs": striped(idx),
    }


def reference(query, keys_words, keys_scales, gout, vals_words, vals_scales, size, dquery, base, offs):
    idx = unstriped(offs)
    keysu = unpack_weight(keys_words, keys_scales, "e2m1")
    valsu = unpack_weight(vals_words, vals_scales, "e2m1")
    queryq = mxq(f64(query), 0, "e4m3")
    keysidxg = keysu[:, idx]
    a = queryq.T @ keysidxg
    dqueryq = mxq(f64(dquery), 0, "e4m3")
    ta = dqueryq.T @ keysidxg
    p = np.exp(a)
    z = np.sum(p, axis=1, keepdims=True)
    p2 = np.square(p)
    s1 = p.reshape(Q, G, I // G).sum(axis=2)
    s2 = p2.reshape(Q, G, I // G).sum(axis=2)
    sh = s1 / s2 / z
    sr = np.repeat(sh, I // G, axis=1)
    goutq = mxq(f64(gout), 0, "e4m3")
    valsidxg = valsu[:, idx]
    c0 = goutq.T @ valsidxg
    dsr = c0 * f64(size) * p2
    dsh = dsr.reshape(Q, G, I // G).sum(axis=2)
    ds2 = dsh / z * s1 / np.square(s2) * (-1.0)
    r1 = np.repeat(ds2, I // G, axis=1)
    ds1 = dsh / z / s2
    r2 = np.repeat(ds1, I // G, axis=1)
    dp2 = c0 * f64(size) * sr + r1
    dz = np.sum(dsh * s1 / s2 / np.square(z) * (-1.0), axis=1, keepdims=True)
    dp = r2 + dp2 * p * 2.0 + dz
    xp = ta * p
    xz = np.sum(xp, axis=1, keepdims=True)
    xp2 = xp * p * 2.0
    xs1 = xp.reshape(Q, G, I // G).sum(axis=2)
    xs2 = xp2.reshape(Q, G, I // G).sum(axis=2)
    xsh = ((xs1 - xs2 * s1 / s2) / s2 - xz * s1 / s2 / z) / z
    xsr = np.repeat(xsh, I // G, axis=1)
    xdsr = xp2 * c0 * f64(size)
    xdsh = xdsr.reshape(Q, G, I // G).sum(axis=2)
    xds2 = ((xdsh - xz * dsh / z) / z * s1 + xs1 * dsh / z - xs2 * s2 * 2.0 * dsh / z * s1 / np.square(s2)) / np.square(s2) * (-1.0)
    xr1 = np.repeat(xds2, I // G, axis=1)
    xds1 = ((xdsh - xz * dsh / z) / z - xs2 * dsh / z / s2) / s2
    xr2 = np.repeat(xds1, I // G, axis=1)
    xdp2 = xsr * c0 * f64(size) + xr1
    xdz = np.sum((xdsh * s1 / s2 + (xs1 - xs2 * s1 / s2) / s2 * dsh - xz * z * 2.0 * dsh * s1 / s2 / np.square(z)) / np.square(z) * (-1.0), axis=1, keepdims=True)
    xdp = xr2 + (xdp2 * p + xp * dp2) * 2.0 + xdz
    xda = xdp * p + xp * dp
    y = xda * 512.0 + f64(base)
    return y

@@ -1,0 +1,323 @@
+from contextlib import ExitStack
+
+import concourse.mybir as mybir
+from concourse.masks import make_identity
+
+D, E, T, I, Q, G = 512, 512, 2048, 512, 128, 64
+J = I // G
+FLOPS = 3 * 2 * D * Q * I
+
+F32 = mybir.dt.float32
+BF16 = mybir.dt.bfloat16
+I32 = mybir.dt.int32
+U32 = mybir.dt.uint32
+U16 = mybir.dt.uint16
+U8 = mybir.dt.uint8
+FP8X4 = mybir.dt.float8_e4m3fn_x4
+FP4X4 = mybir.dt.float4_e2m1fn_x4
+ALU = mybir.AluOpType
+ACT = mybir.ActivationFunctionType
+AX = mybir.AxisListType
+
+P = 128
+PACK = 4
+HALF = G // 2
+OUT_SCALE = 512.0
+SUM_FLOOR = 1e-30
+ROW_FACTORS = (OUT_SCALE, 2 * OUT_SCALE, -OUT_SCALE, -1.0, -0.5)
+
+
+def tile_attend_hvshareofshare_kernel(
+    tc, query, keys_words, keys_scales, gout, vals_words, vals_scales, size, dquery, base, offs, out
+):
+    nc = tc.nc
+    mult, add, sub = ALU.mult, ALU.add, ALU.subtract
+
+    with ExitStack() as ctx:
+        keep = ctx.enter_context(tc.tile_pool(name="keep", bufs=1))
+        psum = ctx.enter_context(tc.psum_pool(name="psum", bufs=1))
+
+        def bank(n, name):
+            return psum.tile([P, I], F32, tag="bank%d" % n, name=name)
+
+        def sb(name, shape, dtype=F32, tag=None):
+            return keep.tile(shape, dtype, name=name, tag=tag or name, align_bytes=64)
+
+        offsets = keep.tile([P, I // 16], U16, name="offsets")
+        k_bytes = sb("k_bytes", [P, T], U8)
+        v_bytes = sb("v_bytes", [P, T], U8)
+        k_words = sb("k_words", [P, T], U16)
+        v_words = sb("v_words", [P, T], U16)
+        warm = sb("warm", [P, 1])
+        warm_out = sb("warm_out", [P, 1])
+        ident = sb("ident", [P, P])
+        factors = sb("factors", [P, len(ROW_FACTORS)])
+        size_col = sb("size_col", [P, 4], tag="q_codes")
+        q_raw = sb("q_raw", [P, PACK, Q], tag="q_then_base")
+        dq_g_raw = sb("dq_g_raw", [P, 2, PACK, Q], tag="rows_then_a")
+
+        nc.vector.memset(k_bytes[:].bitcast(I32), 0)
+        nc.vector.memset(warm[:], 0.0)
+        nc.vector.memset(v_bytes[:].bitcast(I32), 0)
+        make_identity(nc, ident[:])
+        for col, factor in enumerate(ROW_FACTORS):
+            nc.gpsimd.memset(factors[:, col : col + 1], factor)
+
+        def load_scales(tile, scales):
+            for quad in range(4):
+                nc.sync.dma_start(
+                    out=tile[32 * quad : 32 * quad + 4, :].bitcast(I32),
+                    in_=scales[0, 4 * quad : 4 * quad + 4, :].bitcast(I32),
+                )
+
+        def load_rows(raw, rows):
+            nc.sync.dma_start(out=raw, in_=rows.rearrange("(p j) w -> p j w", j=PACK))
+
+        nc.sync.dma_start(offsets[:], offs)
+        nc.sync.dma_start(out=k_words[:].bitcast(I32), in_=keys_words[0].bitcast(I32))
+        nc.sync.dma_start(out=size_col[:], in_=size.rearrange("o (p r) -> (o p) r", r=4))
+        load_rows(q_raw[:], query)
+        load_scales(k_bytes, keys_scales)
+        nc.sync.dma_start(out=v_words[:].bitcast(I32), in_=vals_words[0].bitcast(I32))
+        load_rows(dq_g_raw[:, 0], dquery)
+        load_rows(dq_g_raw[:, 1], gout)
+        load_scales(v_bytes, vals_scales)
+
+        nc.scalar.activation(out=warm_out[:, 0:1], in_=warm[:], func=ACT.Exp)
+
+        def interleave(name, raw):
+            grouped = sb(name, [P, Q, PACK], BF16)
+            nc.scalar.copy(out=grouped[:], in_=raw.rearrange("p j w -> p w j"))
+            return grouped
+
+        def quantize(name, grouped):
+            codes = sb(name + "_codes", [P, Q], U32)
+            scales = sb(name + "_scales", [P, Q], U8)
+            nc.vector.quantize_mx(
+                out=codes[:].bitcast(FP8X4), scales=scales[:], in_=grouped[:].rearrange("p w j -> p (w j)")
+            )
+            return codes, scales
+
+        def gather(name, window, dtype, tag=None):
+            picked = sb(name, [P, I], dtype, tag=tag)
+            nc.vector.tensor_copy(picked[:], window[:].indirect(offsets[:]))
+            return picked
+
+        def scores(acc, rows, words, scale_bytes):
+            nc.tensor.matmul_mx(
+                out=acc[:],
+                lhsT=rows[0][:].bitcast(FP8X4),
+                lhsT_scale=rows[1][:],
+                rhs=words[:].bitcast(FP4X4),
+                rhs_scale=scale_bytes[:],
+                start=True,
+                stop=True,
+            )
+
+        def by_place(acc):
+            return acc[:].rearrange("p (g j) -> p j g", j=J)
+
+        def turn(acc, block, start, stop):
+            nc.tensor.matmul(out=acc, lhsT=block, rhs=ident[:], is_transpose=True, start=start, stop=stop)
+
+        q_bf = interleave("q_bf", q_raw[:])
+        base_sb = sb("base_sb", [P, I], tag="q_then_base")
+        nc.sync.dma_start(out=base_sb[:], in_=base)
+
+        size_ps = bank(3, "size_ps")
+        for r in range(4):
+            turn(size_ps[:, r * P : (r + 1) * P], size_col[:, r : r + 1].to_broadcast([P, P]), True, True)
+        size_j = sb("size_j", [P, J, G])
+        nc.scalar.copy(
+            out=size_j[:].rearrange("p (u r) g -> p u r g", u=2),
+            in_=size_ps[:].rearrange("p (r g u) -> p u r g", r=4, u=2),
+        )
+        dq_bf = interleave("dq_bf", dq_g_raw[:, 0])
+        g_bf = interleave("g_bf", dq_g_raw[:, 1])
+
+        kw = gather("kw", k_words, U16)
+        kb = gather("kb", k_bytes, U8)
+        q_mx = quantize("q", q_bf)
+        a_ps = bank(0, "a_ps")
+        scores(a_ps, q_mx, kw, kb)
+        vw = gather("vw", v_words, U16, tag="q_bf")
+        neg_max = sb("neg_max", [P, 1], tag="v_words")
+        nc.vector.tensor_reduce(out=neg_max[:], in_=a_ps[:], axis=AX.X, op=ALU.max, negate=True)
+        dq_mx = quantize("dq", dq_bf)
+        t_ps = bank(1, "t_ps")
+        scores(t_ps, dq_mx, kw, kb)
+        g_mx = quantize("g", g_bf)
+        vb = gather("vb", v_bytes, U8)
+        c_ps = bank(2, "c_ps")
+        scores(c_ps, g_mx, vw, vb)
+
+        pair_a = sb("pair_a", [P, J, 2, G], tag="rows_then_a")
+        b_and_z = sb("b_and_z", [P, 2 * I + 2], tag="v_bytes")
+        pair_b = b_and_z[:, 0 : 2 * I].rearrange("p (j k g) -> p j k g", j=J, k=2)
+        z, rz = b_and_z[:, 2 * I : 2 * I + 1], b_and_z[:, 2 * I + 1 : 2 * I + 2]
+        pair_c = sb("pair_c", [P, J, 2, G])
+        p, p2 = pair_a[:, :, 0, :], pair_a[:, :, 1, :]
+        p2s = sb("p2s", [P, J, G])
+        z_parts = sb("z_parts", [P, 2])
+        for part in range(2):
+            js = slice(part * J // 2, (part + 1) * J // 2)
+            nc.scalar.activation(
+                out=p[:, js, :],
+                in_=by_place(a_ps)[:, js, :],
+                func=ACT.Exp,
+                bias=neg_max[:],
+                accum_out=z_parts[:, part : part + 1],
+            )
+            nc.scalar.activation(out=p2[:, js, :], in_=p[:, js, :], func=ACT.Square)
+            nc.gpsimd.tensor_tensor(out=p2s[:, js, :], in0=p2[:, js, :], in1=size_j[:, js, :], op=mult)
+
+        xz = sb("xz", [P, 1])
+        t_j = by_place(t_ps)
+        nc.vector.tensor_tensor(out=z, in0=z_parts[:, 0:1], in1=z_parts[:, 1:2], op=add)
+        nc.vector.scalar_tensor_tensor(
+            out=pair_b[:, :, 0, :], in0=t_j, scalar=1.0, in1=p, op0=mult, op1=mult, accum_out=xz[:]
+        )
+        nc.vector.reciprocal(out=rz, in_=z)
+        nc.vector.scalar_tensor_tensor(out=pair_b[:, :, 1, :], in0=t_j, scalar=2.0, in1=p2, op0=mult, op1=mult)
+        nc.vector.tensor_tensor(out=pair_c[:, :, 0, :], in0=by_place(c_ps), in1=p2s[:], op=mult)
+        nc.vector.scalar_tensor_tensor(
+            out=pair_c[:, :, 1, :], in0=t_j, scalar=-2.0, in1=pair_c[:, :, 0, :], op0=mult, op1=mult
+        )
+        rows = sb("rows", [P, len(ROW_FACTORS) + 1])
+        rho, rho2, neg_rho, neg_rz, neg_half_rz, neg_t = [rows[:, col : col + 1] for col in range(len(ROW_FACTORS) + 1)]
+        nc.scalar.activation(out=rows[:, 0 : len(ROW_FACTORS)], in_=factors[:], func=ACT.Copy, scale=rz)
+        nc.scalar.activation(out=neg_t, in_=xz[:], func=ACT.Copy, scale=neg_rz)
+
+        def group_sums(name, pair, turned_ps, sums_ps, floor=0.0):
+            for j in range(J):
+                turn(turned_ps, pair[:, j, :, :].rearrange("p k g -> p (k g)"), j == 0, j == J - 1)
+            turned = sb(name, [P, P])
+            nc.scalar.activation(out=turned[:], in_=turned_ps, func=ACT.Copy, bias=floor)
+            turn(sums_ps, turned[:], True, True)
+
+        sums_a = bank(0, "sums_a")
+        group_sums("turned_a", pair_a, bank(3, "turn_a")[:, 0:P], sums_a[:, 0:P], floor=SUM_FLOOR)
+        w_s1 = sb("w_s1", [P, 2, G])
+        w, neg_s1 = w_s1[:, 0, :], w_s1[:, 1, :]
+        nc.scalar.activation(out=neg_s1, in_=sums_a[:, 0:G], func=ACT.Copy, scale=-1.0)
+        sums_b = bank(4, "sums_b")
+        group_sums("turned_b", pair_b, bank(5, "turn_b")[:, 0:P], sums_b[:, 0:P])
+        base_j = sb("base_j", [P, 2, J, HALF], tag="turned_b")
+        nc.scalar.copy(out=base_j[:], in_=base_sb[:].rearrange("p (h g j) -> p h j g", h=2, j=J))
+        sums_c = bank(6, "sums_c")
+        group_sums("turned_c", pair_c, bank(3, "turn_c")[:, 0:P], sums_c[:, 0:P])
+        slots_a = sb("slots_a", [P, 2, G, J], tag="turned_c")
+        nc.scalar.copy(out=slots_a[:, 0], in_=p.rearrange("p j g -> p g j"))
+        nc.scalar.activation(out=slots_a[:, 1], in_=slots_a[:, 0], func=ACT.Square)
+
+        total_ps = [[bank(1, "total00"), bank(2, "total01")], [bank(7, "total10"), bank(0, "total11")]]
+
+        def add_blocks(blocks, half, start, stop):
+            for jh in range(2):
+                block = blocks[:, 4 * jh : 4 * jh + 4, :].rearrange("p j g -> p (j g)")
+                turn(total_ps[half][jh][:, 0:P], block, start, stop)
+
+        def add_term(name, values, coef, first):
+            terms = sb(name, [P, 2, J, HALF])
+            nc.vector.tensor_tensor(
+                out=terms[:].rearrange("p h j g -> p j h g"),
+                in0=values.rearrange("p j (h g) -> p j h g", h=2),
+                in1=coef.rearrange("p (h g) -> p h g", h=2).unsqueeze(1).to_broadcast([P, J, 2, HALF]),
+                op=mult,
+            )
+            for half in range(2):
+                add_blocks(terms[:, half], half, first, False)
+
+        held = sb("held", [P, 4, G], tag="p2s")
+        coef_c, neg_c_tau = held[:, 0:2, :], held[:, 1:3, :]
+        e, neg_c, tau = held[:, 0, :], held[:, 1, :], held[:, 2, :]
+        r2 = held[:, 3, :]
+        nc.vector.reciprocal(out=r2, in_=sums_a[:, G : 2 * G])
+        nc.vector.scalar_tensor_tensor(out=neg_c, in0=neg_s1, scalar=rho2, in1=r2, op0=mult, op1=mult)
+        nc.vector.tensor_tensor(out=tau, in0=sums_b[:, G : 2 * G], in1=r2, op=mult)
+        add_term("terms_ct", pair_c[:, :, 1, :], neg_c, True)
+        shift = sb("shift", [P, G])
+        nc.vector.scalar_tensor_tensor(out=shift[:], in0=tau, scalar=neg_t, in1=neg_s1, op0=sub, op1=mult)
+        nc.vector.tensor_tensor(out=w, in0=sums_b[:, 0:G], in1=shift[:], op=add)
+        nc.vector.scalar_tensor_tensor(out=e, in0=w, scalar=rho2, in1=r2, op0=mult, op1=mult)
+        add_term("terms_cc", pair_c[:, :, 0, :], e, False)
+        for half in range(2):
+            add_blocks(base_j[:, half], half, False, False)
+
+        def both(ap):
+            return ap.unsqueeze(1).to_broadcast([P, 2, G])
+
+        means = sb("means", [P, 2, G])
+        m, neg_dm = means[:, 0, :], means[:, 1, :]
+        nc.vector.tensor_tensor(
+            out=means[:], in0=sums_c[:, 0:P].rearrange("p (k g) -> p k g", k=2), in1=both(r2), op=mult
+        )
+        scratch = sb("scratch", [P, 3, G])
+        read = sb("read", [P, 1])
+        nc.vector.scalar_tensor_tensor(
+            out=scratch[:, 0, :], in0=sums_c[:, 0:G], scalar=neg_half_rz, in1=neg_c, op0=mult, op1=mult, accum_out=read[:]
+        )
+        b_mtau = sb("b_mtau", [P, 3, G])
+        coef_b, mtau = b_mtau[:, 0:2, :], b_mtau[:, 2, :]
+        nc.vector.tensor_tensor(out=b_mtau[:, 1:3, :], in0=neg_c_tau, in1=both(m), op=mult)
+        nc.vector.tensor_scalar(out=coef_b[:, 0, :], in0=m, scalar1=rho, scalar2=read[:], op0=mult, op1=sub)
+        neg_dread = sb("neg_dread", [P, 1])
+        nc.vector.scalar_tensor_tensor(
+            out=scratch[:, 1:3, :], in0=w_s1[:], scalar=neg_rz, in1=means[:], op0=mult, op1=mult, accum_out=neg_dread[:]
+        )
+
+        def add_b_terms(half):
+            gs = slice(half * HALF, (half + 1) * HALF)
+            terms = sb("terms_b%d" % half, [P, 2, J, HALF])
+            nc.vector.tensor_tensor(
+                out=terms[:].rearrange("p k j g -> p j k g"),
+                in0=pair_b[:, :, :, gs],
+                in1=coef_b[:, :, gs].unsqueeze(1).to_broadcast([P, J, 2, HALF]),
+                op=mult,
+            )
+            for k in range(2):
+                add_blocks(terms[:, k], half, False, k == 1)
+            total = sb("total%d" % half, [P, 2, P])
+            back_ps = bank((5, 3)[half], "back%d" % half)
+            for jh in range(2):
+                nc.scalar.copy(out=total[:, jh, :], in_=total_ps[half][jh][:, 0:P])
+                turn(back_ps[:, jh * P : (jh + 1) * P], total[:, jh, :], True, True)
+            return back_ps
+
+        nc.vector.tensor_tensor(out=neg_dm, in0=neg_dm, in1=mtau, op=add)
+        back = [add_b_terms(0)]
+        ec = sb("ec", [P, 2, G])
+        nc.vector.tensor_tensor(out=ec[:], in0=coef_c, in1=means[:], op=mult)
+        v = sb("v", [P, G])
+        nc.vector.tensor_scalar(out=v[:], in0=neg_dm, scalar1=neg_dread[:], scalar2=neg_rho, op0=sub, op1=mult)
+        back.append(add_b_terms(1))
+        coef_a = sb("coef_a", [P, 2, G])
+        nc.vector.scalar_tensor_tensor(
+            out=coef_a[:, 1, :], in0=ec[:, 0, :], scalar=-1.0, in1=ec[:, 1, :], op0=mult, op1=sub
+        )
+        nc.vector.scalar_tensor_tensor(
+            out=coef_a[:, 0, :], in0=coef_b[:, 0, :], scalar=neg_t, in1=v[:], op0=mult, op1=add
+        )
+
+        terms_a = sb("terms_a", [P, 2, 2, HALF, J])
+        sum_a = sb("sum_a", [P, 2, HALF, J])
+        result = sb("result", [P, 2, HALF, J])
+        for half in range(2):
+            gs = slice(half * HALF, (half + 1) * HALF)
+            nc.vector.tensor_tensor(
+                out=terms_a[:, half],
+                in0=slots_a[:, :, gs, :],
+                in1=coef_a[:, :, gs].unsqueeze(3).to_broadcast([P, 2, HALF, J]),
+                op=mult,
+            )
+        for half in range(2):
+            nc.vector.tensor_tensor(out=sum_a[:, half], in0=terms_a[:, half, 0], in1=terms_a[:, half, 1], op=add)
+        for half in range(2):
+            nc.vector.tensor_tensor(
+                out=result[:, half],
+                in0=back[half][:, 0 : 2 * P].rearrange("p (j g) -> p g j", j=J),
+                in1=sum_a[:, half],
+                op=add,
+            )
+            cols = slice(half * HALF * J, (half + 1) * HALF * J)
+            nc.sync.dma_start(out=out[:, cols], in_=result[:, half].rearrange("p g j -> p (g j)"))

@@ -85,14 +85,13 @@ def tile_attend_hvshareofshare_kernel(
 
         nc.scalar.activation(out=warm_out[:, 0:1], in_=warm[:], func=ACT.Exp)
 
-        def interleave(name, raw):
-            grouped = sb(name, [P, Q, PACK], BF16)
-            nc.scalar.copy(out=grouped[:], in_=raw.rearrange("p j w -> p w j"))
-            return grouped
+        def interleave(grouped, raw):
+            nc.scalar.copy(out=grouped, in_=raw.rearrange("p j w -> p w j"))
 
-        def quantize(name, grouped):
-            codes = sb(name + "_codes", [P, Q], U32)
-            scales = sb(name + "_scales", [P, Q], U8)
+        def quantize(name, grouped, tag):
+            width = grouped.shape[1]
+            codes = sb(name + "_codes", [P, width], U32, tag=tag)
+            scales = sb(name + "_scales", [P, width], U8)
             nc.vector.quantize_mx(
                 out=codes[:].bitcast(FP8X4), scales=scales[:], in_=grouped[:].rearrange("p w j -> p (w j)")
             )
@@ -103,194 +102,181 @@ def tile_attend_hvshareofshare_kernel(
             nc.vector.tensor_copy(picked[:], window[:].indirect(offsets[:]))
             return picked
 
-        def scores(acc, rows, words, scale_bytes):
+        def scores(acc, rows, first, words, scale_bytes):
             nc.tensor.matmul_mx(
                 out=acc[:],
-                lhsT=rows[0][:].bitcast(FP8X4),
-                lhsT_scale=rows[1][:],
+                lhsT=rows[0][:, first : first + Q].bitcast(FP8X4),
+                lhsT_scale=rows[1][:, first : first + Q],
                 rhs=words[:].bitcast(FP4X4),
                 rhs_scale=scale_bytes[:],
                 start=True,
                 stop=True,
             )
 
-        def by_place(acc):
-            return acc[:].rearrange("p (g j) -> p j g", j=J)
-
         def turn(acc, block, start, stop):
             nc.tensor.matmul(out=acc, lhsT=block, rhs=ident[:], is_transpose=True, start=start, stop=stop)
 
-        q_bf = interleave("q_bf", q_raw[:])
+        q_bf = sb("q_bf", [P, Q, PACK], BF16)
+        interleave(q_bf[:], q_raw[:])
         base_sb = sb("base_sb", [P, I], tag="q_then_base")
         nc.sync.dma_start(out=base_sb[:], in_=base)
 
         size_ps = bank(3, "size_ps")
         for r in range(4):
             turn(size_ps[:, r * P : (r + 1) * P], size_col[:, r : r + 1].to_broadcast([P, P]), True, True)
-        size_j = sb("size_j", [P, J, G])
+        size_row = sb("size_row", [P, I])
         nc.scalar.copy(
-            out=size_j[:].rearrange("p (u r) g -> p u r g", u=2),
-            in_=size_ps[:].rearrange("p (r g u) -> p u r g", r=4, u=2),
+            out=size_row[:].rearrange("p (s r) -> p s r", r=4), in_=size_ps[:].rearrange("p (r s) -> p s r", r=4)
         )
-        dq_bf = interleave("dq_bf", dq_g_raw[:, 0])
-        g_bf = interleave("g_bf", dq_g_raw[:, 1])
+        dq_g_bf = sb("dq_g_bf", [P, 2 * Q, PACK], BF16)
+        interleave(dq_g_bf[:, 0:Q, :], dq_g_raw[:, 0])
+        interleave(dq_g_bf[:, Q : 2 * Q, :], dq_g_raw[:, 1])
 
         kw = gather("kw", k_words, U16)
         kb = gather("kb", k_bytes, U8)
-        q_mx = quantize("q", q_bf)
+        q_mx = quantize("q", q_bf, "q_codes")
         a_ps = bank(0, "a_ps")
-        scores(a_ps, q_mx, kw, kb)
+        scores(a_ps, q_mx, 0, kw, kb)
         vw = gather("vw", v_words, U16, tag="q_bf")
-        neg_max = sb("neg_max", [P, 1], tag="v_words")
+        neg_max = sb("neg_max", [P, 1])
         nc.vector.tensor_reduce(out=neg_max[:], in_=a_ps[:], axis=AX.X, op=ALU.max, negate=True)
-        dq_mx = quantize("dq", dq_bf)
+        dq_g_mx = quantize("dq_g", dq_g_bf, "v_words")
         t_ps = bank(1, "t_ps")
-        scores(t_ps, dq_mx, kw, kb)
-        g_mx = quantize("g", g_bf)
+        scores(t_ps, dq_g_mx, 0, kw, kb)
         vb = gather("vb", v_bytes, U8)
         c_ps = bank(2, "c_ps")
-        scores(c_ps, g_mx, vw, vb)
+        scores(c_ps, dq_g_mx, Q, vw, vb)
 
-        pair_a = sb("pair_a", [P, J, 2, G], tag="rows_then_a")
-        b_and_z = sb("b_and_z", [P, 2 * I + 2], tag="v_bytes")
-        pair_b = b_and_z[:, 0 : 2 * I].rearrange("p (j k g) -> p j k g", j=J, k=2)
-        z, rz = b_and_z[:, 2 * I : 2 * I + 1], b_and_z[:, 2 * I + 1 : 2 * I + 2]
-        pair_c = sb("pair_c", [P, J, 2, G])
-        p, p2 = pair_a[:, :, 0, :], pair_a[:, :, 1, :]
-        p2s = sb("p2s", [P, J, G])
-        z_parts = sb("z_parts", [P, 2])
-        for part in range(2):
-            js = slice(part * J // 2, (part + 1) * J // 2)
-            nc.scalar.activation(
-                out=p[:, js, :],
-                in_=by_place(a_ps)[:, js, :],
-                func=ACT.Exp,
-                bias=neg_max[:],
-                accum_out=z_parts[:, part : part + 1],
-            )
-            nc.scalar.activation(out=p2[:, js, :], in_=p[:, js, :], func=ACT.Square)
-            nc.gpsimd.tensor_tensor(out=p2s[:, js, :], in0=p2[:, js, :], in1=size_j[:, js, :], op=mult)
+        pair_a = sb("pair_a", [P, 2, I], tag="rows_then_a")
+        b_and_rz = sb("b_and_rz", [P, 2 * I + 1], tag="v_bytes")
+        pair_b = b_and_rz[:, 0 : 2 * I].rearrange("p (k i) -> p k i", k=2)
+        rz = b_and_rz[:, 2 * I : 2 * I + 1]
+        pair_c = sb("pair_c", [P, 2, I])
+        p, p2 = pair_a[:, 0, :], pair_a[:, 1, :]
+        p2s = sb("p2s", [P, I])
+        z = sb("z", [P, 1], tag="z_then_places")
+        nc.scalar.activation(out=p, in_=a_ps[:], func=ACT.Exp, bias=neg_max[:], accum_out=z[:])
+        nc.scalar.activation(out=p2, in_=p, func=ACT.Square)
+        nc.gpsimd.tensor_tensor(out=p2s[:], in0=p2, in1=size_row[:], op=mult)
 
         xz = sb("xz", [P, 1])
-        t_j = by_place(t_ps)
-        nc.vector.tensor_tensor(out=z, in0=z_parts[:, 0:1], in1=z_parts[:, 1:2], op=add)
+        nc.vector.reciprocal(out=rz, in_=z[:])
         nc.vector.scalar_tensor_tensor(
-            out=pair_b[:, :, 0, :], in0=t_j, scalar=1.0, in1=p, op0=mult, op1=mult, accum_out=xz[:]
+            out=pair_b[:, 0, :], in0=t_ps[:], scalar=1.0, in1=p, op0=mult, op1=mult, accum_out=xz[:]
         )
-        nc.vector.reciprocal(out=rz, in_=z)
-        nc.vector.scalar_tensor_tensor(out=pair_b[:, :, 1, :], in0=t_j, scalar=2.0, in1=p2, op0=mult, op1=mult)
-        nc.vector.tensor_tensor(out=pair_c[:, :, 0, :], in0=by_place(c_ps), in1=p2s[:], op=mult)
+        nc.vector.scalar_tensor_tensor(out=pair_b[:, 1, :], in0=t_ps[:], scalar=2.0, in1=p2, op0=mult, op1=mult)
+        nc.vector.tensor_tensor(out=pair_c[:, 0, :], in0=c_ps[:], in1=p2s[:], op=mult)
         nc.vector.scalar_tensor_tensor(
-            out=pair_c[:, :, 1, :], in0=t_j, scalar=-2.0, in1=pair_c[:, :, 0, :], op0=mult, op1=mult
+            out=pair_c[:, 1, :], in0=t_ps[:], scalar=-2.0, in1=pair_c[:, 0, :], op0=mult, op1=mult
         )
+
+        places = sb("places", [P, J, 2, G], tag="z_then_places")
+        nc.scalar.activation(
+            out=places[:, :, 0, :], in_=a_ps[:].rearrange("p (g j) -> p j g", j=J), func=ACT.Exp, bias=neg_max[:]
+        )
+        nc.scalar.activation(out=places[:, :, 1, :], in_=places[:, :, 0, :], func=ACT.Square)
         rows = sb("rows", [P, len(ROW_FACTORS) + 1])
         rho, rho2, neg_rho, neg_rz, neg_half_rz, neg_t = [rows[:, col : col + 1] for col in range(len(ROW_FACTORS) + 1)]
         nc.scalar.activation(out=rows[:, 0 : len(ROW_FACTORS)], in_=factors[:], func=ACT.Copy, scale=rz)
         nc.scalar.activation(out=neg_t, in_=xz[:], func=ACT.Copy, scale=neg_rz)
-
-        def group_sums(name, pair, turned_ps, sums_ps, floor=0.0):
-            for j in range(J):
-                turn(turned_ps, pair[:, j, :, :].rearrange("p k g -> p (k g)"), j == 0, j == J - 1)
-            turned = sb(name, [P, P])
-            nc.scalar.activation(out=turned[:], in_=turned_ps, func=ACT.Copy, bias=floor)
-            turn(sums_ps, turned[:], True, True)
-
-        sums_a = bank(0, "sums_a")
-        group_sums("turned_a", pair_a, bank(3, "turn_a")[:, 0:P], sums_a[:, 0:P], floor=SUM_FLOOR)
+        turned_ps = bank(3, "turned_ps")
+        for j in range(J):
+            turn(turned_ps[:, 0:P], places[:, j, :, :].rearrange("p k g -> p (k g)"), j == 0, j == J - 1)
+        turned = sb("turned", [P, P])
+        nc.scalar.activation(out=turned[:], in_=turned_ps[:, 0:P], func=ACT.Copy, bias=SUM_FLOOR)
+        sums_a = bank(4, "sums_a")
+        turn(sums_a[:, 0:P], turned[:], True, True)
         w_s1 = sb("w_s1", [P, 2, G])
         w, neg_s1 = w_s1[:, 0, :], w_s1[:, 1, :]
         nc.scalar.activation(out=neg_s1, in_=sums_a[:, 0:G], func=ACT.Copy, scale=-1.0)
-        sums_b = bank(4, "sums_b")
-        group_sums("turned_b", pair_b, bank(5, "turn_b")[:, 0:P], sums_b[:, 0:P])
-        base_j = sb("base_j", [P, 2, J, HALF], tag="turned_b")
-        nc.scalar.copy(out=base_j[:], in_=base_sb[:].rearrange("p (h g j) -> p h j g", h=2, j=J))
-        sums_c = bank(6, "sums_c")
-        group_sums("turned_c", pair_c, bank(3, "turn_c")[:, 0:P], sums_c[:, 0:P])
-        slots_a = sb("slots_a", [P, 2, G, J], tag="turned_c")
-        nc.scalar.copy(out=slots_a[:, 0], in_=p.rearrange("p j g -> p g j"))
-        nc.scalar.activation(out=slots_a[:, 1], in_=slots_a[:, 0], func=ACT.Square)
 
-        total_ps = [[bank(1, "total00"), bank(2, "total01")], [bank(7, "total10"), bank(0, "total11")]]
+        total_ps = [bank(n, "total_ps%d" % n) for n in (5, 6, 7, 0)]
 
-        def add_blocks(blocks, half, start, stop):
-            for jh in range(2):
-                block = blocks[:, 4 * jh : 4 * jh + 4, :].rearrange("p j g -> p (j g)")
-                turn(total_ps[half][jh][:, 0:P], block, start, stop)
+        def add_blocks(terms, blocks, start, stop):
+            for n, block in enumerate(blocks):
+                turn(total_ps[block][:, 0:P], terms[:, n * P : (n + 1) * P], start, stop)
 
-        def add_term(name, values, coef, first):
-            terms = sb(name, [P, 2, J, HALF])
-            nc.vector.tensor_tensor(
-                out=terms[:].rearrange("p h j g -> p j h g"),
-                in0=values.rearrange("p j (h g) -> p j h g", h=2),
-                in1=coef.rearrange("p (h g) -> p h g", h=2).unsqueeze(1).to_broadcast([P, J, 2, HALF]),
-                op=mult,
-            )
-            for half in range(2):
-                add_blocks(terms[:, half], half, first, False)
+        def by_group(ap):
+            return ap.rearrange("p (g j) -> p g j", j=J)
 
-        held = sb("held", [P, 4, G], tag="p2s")
-        coef_c, neg_c_tau = held[:, 0:2, :], held[:, 1:3, :]
-        e, neg_c, tau = held[:, 0, :], held[:, 1, :], held[:, 2, :]
-        r2 = held[:, 3, :]
-        nc.vector.reciprocal(out=r2, in_=sums_a[:, G : 2 * G])
-        nc.vector.scalar_tensor_tensor(out=neg_c, in0=neg_s1, scalar=rho2, in1=r2, op0=mult, op1=mult)
-        nc.vector.tensor_tensor(out=tau, in0=sums_b[:, G : 2 * G], in1=r2, op=mult)
-        add_term("terms_ct", pair_c[:, :, 1, :], neg_c, True)
-        shift = sb("shift", [P, G])
-        nc.vector.scalar_tensor_tensor(out=shift[:], in0=tau, scalar=neg_t, in1=neg_s1, op0=sub, op1=mult)
-        nc.vector.tensor_tensor(out=w, in0=sums_b[:, 0:G], in1=shift[:], op=add)
-        nc.vector.scalar_tensor_tensor(out=e, in0=w, scalar=rho2, in1=r2, op0=mult, op1=mult)
-        add_term("terms_cc", pair_c[:, :, 0, :], e, False)
-        for half in range(2):
-            add_blocks(base_j[:, half], half, False, False)
+        def group_sum(sums, values):
+            nc.vector.tensor_reduce(out=sums, in_=by_group(values), axis=AX.X, op=add)
+
+        def spread(coef):
+            return coef.unsqueeze(len(coef.shape)).to_broadcast(list(coef.shape) + [J])
 
         def both(ap):
             return ap.unsqueeze(1).to_broadcast([P, 2, G])
 
+        def add_term(name, values, coef):
+            terms = sb(name, [P, I])
+            nc.vector.tensor_tensor(out=by_group(terms[:]), in0=by_group(values), in1=spread(coef), op=mult)
+            add_blocks(terms[:], range(4), False, False)
+
+        def pair_terms(name, pair, coef, half):
+            terms = sb("%s%d" % (name, half), [P, 2, HALF, J])
+            nc.vector.tensor_tensor(
+                out=terms[:],
+                in0=pair[:, :, half * HALF * J : (half + 1) * HALF * J].rearrange("p k (g j) -> p k g j", j=J),
+                in1=spread(coef[:, :, half * HALF : (half + 1) * HALF]),
+                op=mult,
+            )
+            return terms
+
+        add_blocks(base_sb[:], range(4), True, False)
+
+        sums_b = sb("sums_b", [P, 2 * G])
+        sums_c = sb("sums_c", [P, 2, G])
+        held = sb("held", [P, 4, G], tag="p2s")
+        coef_c, neg_c_tau = held[:, 0:2, :], held[:, 1:3, :]
+        e, neg_c, tau, r2 = held[:, 0, :], held[:, 1, :], held[:, 2, :], held[:, 3, :]
         means = sb("means", [P, 2, G])
         m, neg_dm = means[:, 0, :], means[:, 1, :]
-        nc.vector.tensor_tensor(
-            out=means[:], in0=sums_c[:, 0:P].rearrange("p (k g) -> p k g", k=2), in1=both(r2), op=mult
-        )
+        shift = sb("shift", [P, G])
         scratch = sb("scratch", [P, 3, G])
         read = sb("read", [P, 1])
-        nc.vector.scalar_tensor_tensor(
-            out=scratch[:, 0, :], in0=sums_c[:, 0:G], scalar=neg_half_rz, in1=neg_c, op0=mult, op1=mult, accum_out=read[:]
-        )
+        neg_dread = sb("neg_dread", [P, 1])
         b_mtau = sb("b_mtau", [P, 3, G])
         coef_b, mtau = b_mtau[:, 0:2, :], b_mtau[:, 2, :]
+
+        group_sum(sums_b[:], pair_b.rearrange("p k i -> p (k i)"))
+        group_sum(sums_c[:, 0, :], pair_c[:, 0, :])
+        nc.vector.reciprocal(out=r2, in_=sums_a[:, G : 2 * G])
+        group_sum(sums_c[:, 1, :], pair_c[:, 1, :])
+        nc.vector.scalar_tensor_tensor(out=neg_c, in0=neg_s1, scalar=rho2, in1=r2, op0=mult, op1=mult)
+        nc.vector.tensor_tensor(out=tau, in0=sums_b[:, G : 2 * G], in1=r2, op=mult)
+        nc.vector.tensor_tensor(out=means[:], in0=sums_c[:], in1=both(r2), op=mult)
+        add_term("terms_ct", pair_c[:, 1, :], neg_c)
+        nc.vector.scalar_tensor_tensor(out=shift[:], in0=tau, scalar=neg_t, in1=neg_s1, op0=sub, op1=mult)
+        nc.vector.scalar_tensor_tensor(
+            out=scratch[:, 0, :], in0=sums_c[:, 0, :], scalar=neg_half_rz, in1=neg_c, op0=mult, op1=mult, accum_out=read[:]
+        )
+        nc.vector.tensor_tensor(out=w, in0=sums_b[:, 0:G], in1=shift[:], op=add)
         nc.vector.tensor_tensor(out=b_mtau[:, 1:3, :], in0=neg_c_tau, in1=both(m), op=mult)
+        nc.vector.scalar_tensor_tensor(out=e, in0=w, scalar=rho2, in1=r2, op0=mult, op1=mult)
         nc.vector.tensor_scalar(out=coef_b[:, 0, :], in0=m, scalar1=rho, scalar2=read[:], op0=mult, op1=sub)
-        neg_dread = sb("neg_dread", [P, 1])
+        add_term("terms_cc", pair_c[:, 0, :], e)
+
+        back_ps = []
+        for half in range(2):
+            terms = pair_terms("terms_b", pair_b, coef_b, half)
+            blocks = (2 * half, 2 * half + 1)
+            for k in range(2):
+                add_blocks(terms[:, k].rearrange("p g j -> p (g j)"), blocks, False, k == 1)
+            total = sb("total%d" % half, [P, 2, P])
+            back_ps.append(bank(1 + half, "back_ps%d" % half))
+            for n, block in enumerate(blocks):
+                nc.scalar.copy(out=total[:, n, :], in_=total_ps[block][:, 0:P])
+                turn(back_ps[half][:, n * P : (n + 1) * P], total[:, n, :], True, True)
+
         nc.vector.scalar_tensor_tensor(
             out=scratch[:, 1:3, :], in0=w_s1[:], scalar=neg_rz, in1=means[:], op0=mult, op1=mult, accum_out=neg_dread[:]
         )
-
-        def add_b_terms(half):
-            gs = slice(half * HALF, (half + 1) * HALF)
-            terms = sb("terms_b%d" % half, [P, 2, J, HALF])
-            nc.vector.tensor_tensor(
-                out=terms[:].rearrange("p k j g -> p j k g"),
-                in0=pair_b[:, :, :, gs],
-                in1=coef_b[:, :, gs].unsqueeze(1).to_broadcast([P, J, 2, HALF]),
-                op=mult,
-            )
-            for k in range(2):
-                add_blocks(terms[:, k], half, False, k == 1)
-            total = sb("total%d" % half, [P, 2, P])
-            back_ps = bank((5, 3)[half], "back%d" % half)
-            for jh in range(2):
-                nc.scalar.copy(out=total[:, jh, :], in_=total_ps[half][jh][:, 0:P])
-                turn(back_ps[:, jh * P : (jh + 1) * P], total[:, jh, :], True, True)
-            return back_ps
-
         nc.vector.tensor_tensor(out=neg_dm, in0=neg_dm, in1=mtau, op=add)
-        back = [add_b_terms(0)]
         ec = sb("ec", [P, 2, G])
         nc.vector.tensor_tensor(out=ec[:], in0=coef_c, in1=means[:], op=mult)
         v = sb("v", [P, G])
         nc.vector.tensor_scalar(out=v[:], in0=neg_dm, scalar1=neg_dread[:], scalar2=neg_rho, op0=sub, op1=mult)
-        back.append(add_b_terms(1))
         coef_a = sb("coef_a", [P, 2, G])
         nc.vector.scalar_tensor_tensor(
             out=coef_a[:, 1, :], in0=ec[:, 0, :], scalar=-1.0, in1=ec[:, 1, :], op0=mult, op1=sub
@@ -299,25 +285,16 @@ def tile_attend_hvshareofshare_kernel(
             out=coef_a[:, 0, :], in0=coef_b[:, 0, :], scalar=neg_t, in1=v[:], op0=mult, op1=add
         )
 
-        terms_a = sb("terms_a", [P, 2, 2, HALF, J])
+        terms_a = [pair_terms("terms_a", pair_a, coef_a, half) for half in range(2)]
         sum_a = sb("sum_a", [P, 2, HALF, J])
-        result = sb("result", [P, 2, HALF, J])
+        result = sb("result", [P, 2, HALF * J])
         for half in range(2):
-            gs = slice(half * HALF, (half + 1) * HALF)
-            nc.vector.tensor_tensor(
-                out=terms_a[:, half],
-                in0=slots_a[:, :, gs, :],
-                in1=coef_a[:, :, gs].unsqueeze(3).to_broadcast([P, 2, HALF, J]),
-                op=mult,
-            )
-        for half in range(2):
-            nc.vector.tensor_tensor(out=sum_a[:, half], in0=terms_a[:, half, 0], in1=terms_a[:, half, 1], op=add)
+            nc.vector.tensor_tensor(out=sum_a[:, half], in0=terms_a[half][:, 0], in1=terms_a[half][:, 1], op=add)
         for half in range(2):
             nc.vector.tensor_tensor(
                 out=result[:, half],
-                in0=back[half][:, 0 : 2 * P].rearrange("p (j g) -> p g j", j=J),
-                in1=sum_a[:, half],
+                in0=back_ps[half][:, 0 : 2 * P],
+                in1=sum_a[:, half].rearrange("p g j -> p (g j)"),
                 op=add,
             )
-            cols = slice(half * HALF * J, (half + 1) * HALF * J)
-            nc.sync.dma_start(out=out[:, cols], in_=result[:, half].rearrange("p g j -> p (g j)"))
+            nc.sync.dma_start(out=out[:, half * HALF * J : (half + 1) * HALF * J], in_=result[:, half])

@@ -48,8 +48,8 @@ def tile_attend_hvshareofshare_kernel(
         v_bytes = sb("v_bytes", [P, T], U8)
         k_words = sb("k_words", [P, T], U16)
         v_words = sb("v_words", [P, T], U16)
-        warm = sb("warm", [P, 1])
-        warm_out = sb("warm_out", [P, 1])
+        warm = sb("warm", [P, 1], tag="zero_then_places")
+        warm_out = sb("warm_out", [P, 2])
         ident = sb("ident", [P, P])
         factors = sb("factors", [P, len(ROW_FACTORS)])
         size_col = sb("size_col", [P, 4], tag="q_codes")
@@ -154,9 +154,9 @@ def tile_attend_hvshareofshare_kernel(
         pair_c = sb("pair_c", [P, 2, I])
         p, p2 = pair_a[:, 0, :], pair_a[:, 1, :]
         p2s = sb("p2s", [P, I])
-        z = sb("z", [P, 1], tag="z_then_places")
+        z = sb("z", [P, 1])
         nc.scalar.activation(out=p, in_=a_ps[:], func=ACT.Exp, bias=neg_max[:], accum_out=z[:])
-        nc.scalar.activation(out=p2, in_=p, func=ACT.Square)
+        nc.scalar.activation(out=p2, in_=p, func=ACT.Square, bias=warm[:])
         nc.gpsimd.tensor_tensor(out=p2s[:], in0=p2, in1=size_row[:], op=mult)
 
         xz = sb("xz", [P, 1])
@@ -170,7 +170,7 @@ def tile_attend_hvshareofshare_kernel(
             out=pair_c[:, 1, :], in0=t_ps[:], scalar=-2.0, in1=pair_c[:, 0, :], op0=mult, op1=mult
         )
 
-        places = sb("places", [P, J, 2, G], tag="z_then_places")
+        places = sb("places", [P, J, 2, G], tag="zero_then_places")
         nc.scalar.activation(
             out=places[:, :, 0, :], in_=a_ps[:].rearrange("p (g j) -> p j g", j=J), func=ACT.Exp, bias=neg_max[:]
         )
@@ -179,6 +179,7 @@ def tile_attend_hvshareofshare_kernel(
         rho, rho2, neg_rho, neg_rz, neg_half_rz, neg_t = [rows[:, col : col + 1] for col in range(len(ROW_FACTORS) + 1)]
         nc.scalar.activation(out=rows[:, 0 : len(ROW_FACTORS)], in_=factors[:], func=ACT.Copy, scale=rz)
         nc.scalar.activation(out=neg_t, in_=xz[:], func=ACT.Copy, scale=neg_rz)
+        nc.scalar.activation(out=warm_out[:, 1:2], in_=places[:, J - 1, 1, 0:1], func=ACT.Abs_reciprocal_sqrt)
         turned_ps = bank(3, "turned_ps")
         for j in range(J):
             turn(turned_ps[:, 0:P], places[:, j, :, :].rearrange("p k g -> p (k g)"), j == 0, j == J - 1)
@@ -188,7 +189,11 @@ def tile_attend_hvshareofshare_kernel(
         turn(sums_a[:, 0:P], turned[:], True, True)
         w_s1 = sb("w_s1", [P, 2, G])
         w, neg_s1 = w_s1[:, 0, :], w_s1[:, 1, :]
+        root_r2 = sb("root_r2", [P, 2, G])
+        root, r2 = root_r2[:, 0, :], root_r2[:, 1, :]
+        nc.scalar.activation(out=root, in_=sums_a[:, G : 2 * G], func=ACT.Abs_reciprocal_sqrt)
         nc.scalar.activation(out=neg_s1, in_=sums_a[:, 0:G], func=ACT.Copy, scale=-1.0)
+        nc.scalar.activation(out=r2, in_=root, func=ACT.Square)
 
         total_ps = [bank(n, "total_ps%d" % n) for n in (5, 6, 7, 0)]
 
@@ -200,7 +205,13 @@ def tile_attend_hvshareofshare_kernel(
             return ap.rearrange("p (g j) -> p g j", j=J)
 
         def group_sum(sums, values):
-            nc.vector.tensor_reduce(out=sums, in_=by_group(values), axis=AX.X, op=add)
+            nc.vector.tensor_reduce(out=sums, in_=values, axis=AX.X, op=add)
+
+        def fold(name, values):
+            grouped = by_group(values)
+            folded = sb(name, [P, grouped.shape[1], J // 2])
+            nc.gpsimd.tensor_tensor(out=folded[:], in0=grouped[:, :, 0 : J // 2], in1=grouped[:, :, J // 2 : J], op=add)
+            return folded
 
         def spread(coef):
             return coef.unsqueeze(len(coef.shape)).to_broadcast(list(coef.shape) + [J])
@@ -227,9 +238,9 @@ def tile_attend_hvshareofshare_kernel(
 
         sums_b = sb("sums_b", [P, 2 * G])
         sums_c = sb("sums_c", [P, 2, G])
-        held = sb("held", [P, 4, G], tag="p2s")
+        held = sb("held", [P, 3, G], tag="p2s")
         coef_c, neg_c_tau = held[:, 0:2, :], held[:, 1:3, :]
-        e, neg_c, tau, r2 = held[:, 0, :], held[:, 1, :], held[:, 2, :], held[:, 3, :]
+        e, neg_c, tau = held[:, 0, :], held[:, 1, :], held[:, 2, :]
         means = sb("means", [P, 2, G])
         m, neg_dm = means[:, 0, :], means[:, 1, :]
         shift = sb("shift", [P, G])
@@ -239,10 +250,10 @@ def tile_attend_hvshareofshare_kernel(
         b_mtau = sb("b_mtau", [P, 3, G])
         coef_b, mtau = b_mtau[:, 0:2, :], b_mtau[:, 2, :]
 
-        group_sum(sums_b[:], pair_b.rearrange("p k i -> p (k i)"))
-        group_sum(sums_c[:, 0, :], pair_c[:, 0, :])
-        nc.vector.reciprocal(out=r2, in_=sums_a[:, G : 2 * G])
-        group_sum(sums_c[:, 1, :], pair_c[:, 1, :])
+        folded_b = fold("folded_b", pair_b.rearrange("p k i -> p (k i)"))
+        group_sum(sums_c[:, 0, :], by_group(pair_c[:, 0, :]))
+        group_sum(sums_c[:, 1, :], by_group(pair_c[:, 1, :]))
+        group_sum(sums_b[:], folded_b[:])
         nc.vector.scalar_tensor_tensor(out=neg_c, in0=neg_s1, scalar=rho2, in1=r2, op0=mult, op1=mult)
         nc.vector.tensor_tensor(out=tau, in0=sums_b[:, G : 2 * G], in1=r2, op=mult)
         nc.vector.tensor_tensor(out=means[:], in0=sums_c[:], in1=both(r2), op=mult)
@@ -255,7 +266,11 @@ def tile_attend_hvshareofshare_kernel(
         nc.vector.tensor_tensor(out=b_mtau[:, 1:3, :], in0=neg_c_tau, in1=both(m), op=mult)
         nc.vector.scalar_tensor_tensor(out=e, in0=w, scalar=rho2, in1=r2, op0=mult, op1=mult)
         nc.vector.tensor_scalar(out=coef_b[:, 0, :], in0=m, scalar1=rho, scalar2=read[:], op0=mult, op1=sub)
+        nc.vector.scalar_tensor_tensor(
+            out=scratch[:, 1:3, :], in0=w_s1[:], scalar=neg_rz, in1=means[:], op0=mult, op1=mult, accum_out=neg_dread[:]
+        )
         add_term("terms_cc", pair_c[:, 0, :], e)
+        nc.vector.tensor_tensor(out=neg_dm, in0=neg_dm, in1=mtau, op=add)
 
         back_ps = []
         for half in range(2):
@@ -269,10 +284,6 @@ def tile_attend_hvshareofshare_kernel(
                 nc.scalar.copy(out=total[:, n, :], in_=total_ps[block][:, 0:P])
                 turn(back_ps[half][:, n * P : (n + 1) * P], total[:, n, :], True, True)
 
-        nc.vector.scalar_tensor_tensor(
-            out=scratch[:, 1:3, :], in0=w_s1[:], scalar=neg_rz, in1=means[:], op0=mult, op1=mult, accum_out=neg_dread[:]
-        )
-        nc.vector.tensor_tensor(out=neg_dm, in0=neg_dm, in1=mtau, op=add)
         ec = sb("ec", [P, 2, G])
         nc.vector.tensor_tensor(out=ec[:], in0=coef_c, in1=means[:], op=mult)
         v = sb("v", [P, G])

@@ -3,9 +3,9 @@ from contextlib import ExitStack
 import concourse.mybir as mybir
 from concourse.masks import make_identity
 
-D, E, T, I, Q, G = 512, 512, 2048, 512, 128, 64
-J = I // G
-FLOPS = 3 * 2 * D * Q * I
+FEATURES, TOKENS, SLOTS, ROWS, GROUPS = 512, 2048, 512, 128, 64
+PER_GROUP = SLOTS // GROUPS
+FLOPS = 3 * 2 * FEATURES * ROWS * SLOTS
 
 F32 = mybir.dt.float32
 BF16 = mybir.dt.bfloat16
@@ -21,7 +21,10 @@ AX = mybir.AxisListType
 
 P = 128
 PACK = 4
-HALF = G // 2
+QUADRANTS, SCALE_ROWS = 4, 4
+SIZE_COLS = SLOTS // P
+BLOCKS = SLOTS // P
+HALF_SLOTS, HALF_GROUPS = SLOTS // 2, GROUPS // 2
 OUT_SCALE = 512.0
 SUM_FLOOR = 1e-30
 ROW_FACTORS = (OUT_SCALE, 2 * OUT_SCALE, -OUT_SCALE, -1.0, -0.5)
@@ -38,44 +41,44 @@ def tile_attend_hvshareofshare_kernel(
         psum = ctx.enter_context(tc.psum_pool(name="psum", bufs=1))
 
         def bank(n, name):
-            return psum.tile([P, I], F32, tag="bank%d" % n, name=name)
+            return psum.tile([P, SLOTS], F32, tag="bank%d" % n, name=name)
 
         def sb(name, shape, dtype=F32, tag=None):
             return keep.tile(shape, dtype, name=name, tag=tag or name, align_bytes=64)
 
-        offsets = keep.tile([P, I // 16], U16, name="offsets")
-        k_bytes = sb("k_bytes", [P, T], U8)
-        v_bytes = sb("v_bytes", [P, T], U8)
-        k_words = sb("k_words", [P, T], U16)
-        v_words = sb("v_words", [P, T], U16)
-        warm = sb("warm", [P, 1], tag="zero_then_places")
-        warm_out = sb("warm_out", [P, 2])
+        offsets = keep.tile([P, SLOTS // 16], U16, name="offsets")
+        k_bytes = sb("k_bytes", [P, TOKENS], U8)
+        v_bytes = sb("v_bytes", [P, TOKENS], U8)
+        k_words = sb("k_words", [P, TOKENS], U16)
+        v_words = sb("v_words", [P, TOKENS], U16)
+        zero = sb("zero", [P, 1], tag="zero_then_places")
+        one = sb("one", [P, 1])
         ident = sb("ident", [P, P])
         factors = sb("factors", [P, len(ROW_FACTORS)])
-        size_col = sb("size_col", [P, 4], tag="q_codes")
-        q_raw = sb("q_raw", [P, PACK, Q], tag="q_then_base")
-        dq_g_raw = sb("dq_g_raw", [P, 2, PACK, Q], tag="rows_then_a")
+        size_col = sb("size_col", [P, SIZE_COLS], tag="size_then_q_codes")
+        q_raw = sb("q_raw", [P, PACK, ROWS], tag="q_then_base")
+        dq_g_raw = sb("dq_g_raw", [P, 2, PACK, ROWS], tag="rows_then_p")
 
         nc.vector.memset(k_bytes[:].bitcast(I32), 0)
-        nc.vector.memset(warm[:], 0.0)
+        nc.vector.memset(zero[:], 0.0)
         nc.vector.memset(v_bytes[:].bitcast(I32), 0)
         make_identity(nc, ident[:])
         for col, factor in enumerate(ROW_FACTORS):
             nc.gpsimd.memset(factors[:, col : col + 1], factor)
 
         def load_scales(tile, scales):
-            for quad in range(4):
+            for quad in range(QUADRANTS):
                 nc.sync.dma_start(
-                    out=tile[32 * quad : 32 * quad + 4, :].bitcast(I32),
-                    in_=scales[0, 4 * quad : 4 * quad + 4, :].bitcast(I32),
+                    out=tile[32 * quad : 32 * quad + SCALE_ROWS, :].bitcast(I32),
+                    in_=scales[0, SCALE_ROWS * quad : SCALE_ROWS * (quad + 1), :].bitcast(I32),
                 )
 
-        def load_rows(raw, rows):
-            nc.sync.dma_start(out=raw, in_=rows.rearrange("(p j) w -> p j w", j=PACK))
+        def load_rows(raw, source):
+            nc.sync.dma_start(out=raw, in_=source.rearrange("(p r) w -> p r w", r=PACK))
 
         nc.sync.dma_start(offsets[:], offs)
         nc.sync.dma_start(out=k_words[:].bitcast(I32), in_=keys_words[0].bitcast(I32))
-        nc.sync.dma_start(out=size_col[:], in_=size.rearrange("o (p r) -> (o p) r", r=4))
+        nc.sync.dma_start(out=size_col[:], in_=size.rearrange("o (p r) -> (o p) r", r=SIZE_COLS))
         load_rows(q_raw[:], query)
         load_scales(k_bytes, keys_scales)
         nc.sync.dma_start(out=v_words[:].bitcast(I32), in_=vals_words[0].bitcast(I32))
@@ -83,30 +86,31 @@ def tile_attend_hvshareofshare_kernel(
         load_rows(dq_g_raw[:, 1], gout)
         load_scales(v_bytes, vals_scales)
 
-        nc.scalar.activation(out=warm_out[:, 0:1], in_=warm[:], func=ACT.Exp)
+        nc.scalar.activation(out=one[:], in_=zero[:], func=ACT.Exp)
 
         def interleave(grouped, raw):
-            nc.scalar.copy(out=grouped, in_=raw.rearrange("p j w -> p w j"))
+            nc.scalar.copy(out=grouped, in_=raw.rearrange("p r w -> p w r"))
 
         def quantize(name, grouped, tag):
             width = grouped.shape[1]
             codes = sb(name + "_codes", [P, width], U32, tag=tag)
             scales = sb(name + "_scales", [P, width], U8)
             nc.vector.quantize_mx(
-                out=codes[:].bitcast(FP8X4), scales=scales[:], in_=grouped[:].rearrange("p w j -> p (w j)")
+                out=codes[:].bitcast(FP8X4), scales=scales[:], in_=grouped[:].rearrange("p w r -> p (w r)")
             )
             return codes, scales
 
         def gather(name, window, dtype, tag=None):
-            picked = sb(name, [P, I], dtype, tag=tag)
+            picked = sb(name, [P, SLOTS], dtype, tag=tag)
             nc.vector.tensor_copy(picked[:], window[:].indirect(offsets[:]))
             return picked
 
-        def scores(acc, rows, first, words, scale_bytes):
+        def scores(acc, quantized, first, words, scale_bytes):
+            codes, scales = quantized
             nc.tensor.matmul_mx(
                 out=acc[:],
-                lhsT=rows[0][:, first : first + Q].bitcast(FP8X4),
-                lhsT_scale=rows[1][:, first : first + Q],
+                lhsT=codes[:, first : first + ROWS].bitcast(FP8X4),
+                lhsT_scale=scales[:, first : first + ROWS],
                 rhs=words[:].bitcast(FP4X4),
                 rhs_scale=scale_bytes[:],
                 start=True,
@@ -116,196 +120,212 @@ def tile_attend_hvshareofshare_kernel(
         def turn(acc, block, start, stop):
             nc.tensor.matmul(out=acc, lhsT=block, rhs=ident[:], is_transpose=True, start=start, stop=stop)
 
-        q_bf = sb("q_bf", [P, Q, PACK], BF16)
+        q_bf = sb("q_bf", [P, ROWS, PACK], BF16, tag="q_bf_then_v_picked")
         interleave(q_bf[:], q_raw[:])
-        base_sb = sb("base_sb", [P, I], tag="q_then_base")
+        base_sb = sb("base_sb", [P, SLOTS], tag="q_then_base")
         nc.sync.dma_start(out=base_sb[:], in_=base)
 
         size_ps = bank(3, "size_ps")
-        for r in range(4):
+        for r in range(SIZE_COLS):
             turn(size_ps[:, r * P : (r + 1) * P], size_col[:, r : r + 1].to_broadcast([P, P]), True, True)
-        size_row = sb("size_row", [P, I])
-        nc.scalar.copy(
-            out=size_row[:].rearrange("p (s r) -> p s r", r=4), in_=size_ps[:].rearrange("p (r s) -> p s r", r=4)
+        size_row = sb("size_row", [P, SLOTS])
+        nc.scalar.activation(
+            out=size_row[:].rearrange("p (s r) -> p s r", r=SIZE_COLS),
+            in_=size_ps[:].rearrange("p (r s) -> p s r", r=SIZE_COLS),
+            func=ACT.Copy,
+            scale=one[:],
         )
-        dq_g_bf = sb("dq_g_bf", [P, 2 * Q, PACK], BF16)
-        interleave(dq_g_bf[:, 0:Q, :], dq_g_raw[:, 0])
-        interleave(dq_g_bf[:, Q : 2 * Q, :], dq_g_raw[:, 1])
+        dq_g_bf = sb("dq_g_bf", [P, 2 * ROWS, PACK], BF16)
+        interleave(dq_g_bf[:, 0:ROWS, :], dq_g_raw[:, 0])
+        interleave(dq_g_bf[:, ROWS : 2 * ROWS, :], dq_g_raw[:, 1])
 
-        kw = gather("kw", k_words, U16)
-        kb = gather("kb", k_bytes, U8)
-        q_mx = quantize("q", q_bf, "q_codes")
+        k_words_picked = gather("k_words_picked", k_words, U16)
+        k_bytes_picked = gather("k_bytes_picked", k_bytes, U8)
+        q_mx = quantize("q", q_bf, "size_then_q_codes")
         a_ps = bank(0, "a_ps")
-        scores(a_ps, q_mx, 0, kw, kb)
-        vw = gather("vw", v_words, U16, tag="q_bf")
+        scores(a_ps, q_mx, 0, k_words_picked, k_bytes_picked)
+        v_words_picked = gather("v_words_picked", v_words, U16, tag="q_bf_then_v_picked")
         neg_max = sb("neg_max", [P, 1])
         nc.vector.tensor_reduce(out=neg_max[:], in_=a_ps[:], axis=AX.X, op=ALU.max, negate=True)
         dq_g_mx = quantize("dq_g", dq_g_bf, "v_words")
         t_ps = bank(1, "t_ps")
-        scores(t_ps, dq_g_mx, 0, kw, kb)
-        vb = gather("vb", v_bytes, U8)
+        scores(t_ps, dq_g_mx, 0, k_words_picked, k_bytes_picked)
+        v_bytes_picked = gather("v_bytes_picked", v_bytes, U8)
         c_ps = bank(2, "c_ps")
-        scores(c_ps, dq_g_mx, Q, vw, vb)
+        scores(c_ps, dq_g_mx, ROWS, v_words_picked, v_bytes_picked)
 
-        pair_a = sb("pair_a", [P, 2, I], tag="rows_then_a")
-        b_and_rz = sb("b_and_rz", [P, 2 * I + 1], tag="v_bytes")
-        pair_b = b_and_rz[:, 0 : 2 * I].rearrange("p (k i) -> p k i", k=2)
-        rz = b_and_rz[:, 2 * I : 2 * I + 1]
-        pair_c = sb("pair_c", [P, 2, I])
-        p, p2 = pair_a[:, 0, :], pair_a[:, 1, :]
-        p2s = sb("p2s", [P, I])
+        pair_p = sb("pair_p", [P, 2, SLOTS], tag="rows_then_p")
+        t_and_rz = sb("t_and_rz", [P, 2 * SLOTS + 1], tag="v_bytes")
+        pair_t = t_and_rz[:, 0 : 2 * SLOTS].rearrange("p (k i) -> p k i", k=2)
+        rz = t_and_rz[:, 2 * SLOTS : 2 * SLOTS + 1]
+        pair_c = sb("pair_c", [P, 2, SLOTS])
+        p, p2 = pair_p[:, 0, :], pair_p[:, 1, :]
+        p2_size = sb("p2_size", [P, SLOTS], tag="p2_size_then_coefs")
         z = sb("z", [P, 1])
         nc.scalar.activation(out=p, in_=a_ps[:], func=ACT.Exp, bias=neg_max[:], accum_out=z[:])
-        nc.scalar.activation(out=p2, in_=p, func=ACT.Square, bias=warm[:])
-        nc.gpsimd.tensor_tensor(out=p2s[:], in0=p2, in1=size_row[:], op=mult)
+        nc.scalar.activation(out=p2, in_=p, func=ACT.Square, bias=zero[:])
+        nc.gpsimd.tensor_tensor(out=p2_size[:], in0=p2, in1=size_row[:], op=mult)
 
         xz = sb("xz", [P, 1])
         nc.vector.reciprocal(out=rz, in_=z[:])
         nc.vector.scalar_tensor_tensor(
-            out=pair_b[:, 0, :], in0=t_ps[:], scalar=1.0, in1=p, op0=mult, op1=mult, accum_out=xz[:]
+            out=pair_t[:, 0, :], in0=t_ps[:], scalar=1.0, in1=p, op0=mult, op1=mult, accum_out=xz[:]
         )
-        nc.vector.scalar_tensor_tensor(out=pair_b[:, 1, :], in0=t_ps[:], scalar=2.0, in1=p2, op0=mult, op1=mult)
-        nc.vector.tensor_tensor(out=pair_c[:, 0, :], in0=c_ps[:], in1=p2s[:], op=mult)
+        nc.vector.scalar_tensor_tensor(out=pair_t[:, 1, :], in0=t_ps[:], scalar=2.0, in1=p2, op0=mult, op1=mult)
+        nc.vector.tensor_tensor(out=pair_c[:, 0, :], in0=c_ps[:], in1=p2_size[:], op=mult)
         nc.vector.scalar_tensor_tensor(
             out=pair_c[:, 1, :], in0=t_ps[:], scalar=-2.0, in1=pair_c[:, 0, :], op0=mult, op1=mult
         )
 
-        places = sb("places", [P, J, 2, G], tag="zero_then_places")
+        places = sb("places", [P, PER_GROUP, 2, GROUPS], tag="zero_then_places")
         nc.scalar.activation(
-            out=places[:, :, 0, :], in_=a_ps[:].rearrange("p (g j) -> p j g", j=J), func=ACT.Exp, bias=neg_max[:]
+            out=places[:, :, 0, :],
+            in_=a_ps[:].rearrange("p (g j) -> p j g", j=PER_GROUP),
+            func=ACT.Exp,
+            bias=neg_max[:],
         )
         nc.scalar.activation(out=places[:, :, 1, :], in_=places[:, :, 0, :], func=ACT.Square)
-        rows = sb("rows", [P, len(ROW_FACTORS) + 1])
-        rho, rho2, neg_rho, neg_rz, neg_half_rz, neg_t = [rows[:, col : col + 1] for col in range(len(ROW_FACTORS) + 1)]
-        nc.scalar.activation(out=rows[:, 0 : len(ROW_FACTORS)], in_=factors[:], func=ACT.Copy, scale=rz)
-        nc.scalar.activation(out=neg_t, in_=xz[:], func=ACT.Copy, scale=neg_rz)
-        nc.scalar.activation(out=warm_out[:, 1:2], in_=places[:, J - 1, 1, 0:1], func=ACT.Abs_reciprocal_sqrt)
+        row_scalars = sb("row_scalars", [P, len(ROW_FACTORS) + 1])
+        rho, rho2, neg_rho, neg_rz, neg_half_rz, neg_tbar = [
+            row_scalars[:, col : col + 1] for col in range(len(ROW_FACTORS) + 1)
+        ]
+        nc.scalar.activation(out=row_scalars[:, 0 : len(ROW_FACTORS)], in_=factors[:], func=ACT.Copy, scale=rz)
+        nc.scalar.activation(out=neg_tbar, in_=xz[:], func=ACT.Copy, scale=neg_rz)
         turned_ps = bank(3, "turned_ps")
-        for j in range(J):
-            turn(turned_ps[:, 0:P], places[:, j, :, :].rearrange("p k g -> p (k g)"), j == 0, j == J - 1)
+        for j in range(PER_GROUP):
+            turn(turned_ps[:, 0:P], places[:, j, :, :].rearrange("p k g -> p (k g)"), j == 0, j == PER_GROUP - 1)
         turned = sb("turned", [P, P])
         nc.scalar.activation(out=turned[:], in_=turned_ps[:, 0:P], func=ACT.Copy, bias=SUM_FLOOR)
-        sums_a = bank(4, "sums_a")
-        turn(sums_a[:, 0:P], turned[:], True, True)
-        w_s1 = sb("w_s1", [P, 2, G])
-        w, neg_s1 = w_s1[:, 0, :], w_s1[:, 1, :]
-        root_r2 = sb("root_r2", [P, 2, G])
-        root, r2 = root_r2[:, 0, :], root_r2[:, 1, :]
-        nc.scalar.activation(out=root, in_=sums_a[:, G : 2 * G], func=ACT.Abs_reciprocal_sqrt)
-        nc.scalar.activation(out=neg_s1, in_=sums_a[:, 0:G], func=ACT.Copy, scale=-1.0)
-        nc.scalar.activation(out=r2, in_=root, func=ACT.Square)
+        sums_p = bank(4, "sums_p")
+        turn(sums_p[:, 0:P], turned[:], True, True)
 
         total_ps = [bank(n, "total_ps%d" % n) for n in (5, 6, 7, 0)]
 
-        def add_blocks(terms, blocks, start, stop):
-            for n, block in enumerate(blocks):
-                turn(total_ps[block][:, 0:P], terms[:, n * P : (n + 1) * P], start, stop)
+        def add_blocks(terms, start):
+            for block in range(BLOCKS):
+                turn(total_ps[block][:, 0:P], terms[:, block * P : (block + 1) * P], start, False)
 
         def by_group(ap):
-            return ap.rearrange("p (g j) -> p g j", j=J)
+            return ap.rearrange("p (g j) -> p g j", j=PER_GROUP)
 
         def group_sum(sums, values):
             nc.vector.tensor_reduce(out=sums, in_=values, axis=AX.X, op=add)
 
-        def fold(name, values):
-            grouped = by_group(values)
-            folded = sb(name, [P, grouped.shape[1], J // 2])
-            nc.gpsimd.tensor_tensor(out=folded[:], in0=grouped[:, :, 0 : J // 2], in1=grouped[:, :, J // 2 : J], op=add)
-            return folded
-
         def spread(coef):
-            return coef.unsqueeze(len(coef.shape)).to_broadcast(list(coef.shape) + [J])
+            return coef.unsqueeze(len(coef.shape)).to_broadcast(list(coef.shape) + [PER_GROUP])
 
         def both(ap):
-            return ap.unsqueeze(1).to_broadcast([P, 2, G])
+            return ap.unsqueeze(1).to_broadcast([P, 2, GROUPS])
 
         def add_term(name, values, coef):
-            terms = sb(name, [P, I])
+            terms = sb(name, [P, SLOTS])
             nc.vector.tensor_tensor(out=by_group(terms[:]), in0=by_group(values), in1=spread(coef), op=mult)
-            add_blocks(terms[:], range(4), False, False)
+            add_blocks(terms[:], False)
 
         def pair_terms(name, pair, coef, half):
-            terms = sb("%s%d" % (name, half), [P, 2, HALF, J])
+            terms = sb("%s%d" % (name, half), [P, 2, HALF_GROUPS, PER_GROUP])
             nc.vector.tensor_tensor(
                 out=terms[:],
-                in0=pair[:, :, half * HALF * J : (half + 1) * HALF * J].rearrange("p k (g j) -> p k g j", j=J),
-                in1=spread(coef[:, :, half * HALF : (half + 1) * HALF]),
+                in0=pair[:, :, half * HALF_SLOTS : (half + 1) * HALF_SLOTS].rearrange(
+                    "p k (g j) -> p k g j", j=PER_GROUP
+                ),
+                in1=spread(coef[:, :, half * HALF_GROUPS : (half + 1) * HALF_GROUPS]),
                 op=mult,
             )
             return terms
 
-        add_blocks(base_sb[:], range(4), True, False)
+        add_blocks(base_sb[:], True)
 
-        sums_b = sb("sums_b", [P, 2 * G])
-        sums_c = sb("sums_c", [P, 2, G])
-        held = sb("held", [P, 3, G], tag="p2s")
-        coef_c, neg_c_tau = held[:, 0:2, :], held[:, 1:3, :]
-        e, neg_c, tau = held[:, 0, :], held[:, 1, :], held[:, 2, :]
-        means = sb("means", [P, 2, G])
+        sums_t = sb("sums_t", [P, 2 * GROUPS])
+        sums_c = sb("sums_c", [P, 2, GROUPS])
+        coefs = sb("coefs", [P, 4, GROUPS], tag="p2_size_then_coefs")
+        coef_c, neg_kc_tau = coefs[:, 0:2, :], coefs[:, 1:3, :]
+        ke, neg_kc, tau, r2 = coefs[:, 0, :], coefs[:, 1, :], coefs[:, 2, :], coefs[:, 3, :]
+        w_s1 = sb("w_s1", [P, 2, GROUPS])
+        w, neg_s1 = w_s1[:, 0, :], w_s1[:, 1, :]
+        means = sb("means", [P, 2, GROUPS])
         m, neg_dm = means[:, 0, :], means[:, 1, :]
-        shift = sb("shift", [P, G])
-        scratch = sb("scratch", [P, 3, G])
-        read = sb("read", [P, 1])
-        neg_dread = sb("neg_dread", [P, 1])
-        b_mtau = sb("b_mtau", [P, 3, G])
-        coef_b, mtau = b_mtau[:, 0:2, :], b_mtau[:, 2, :]
+        shift = sb("shift", [P, GROUPS])
+        summands = sb("summands", [P, 3, GROUPS])
+        rho_f = sb("rho_f", [P, 1])
+        neg_df = sb("neg_df", [P, 1])
+        t_mtau = sb("t_mtau", [P, 3, GROUPS])
+        coef_t, mtau = t_mtau[:, 0:2, :], t_mtau[:, 2, :]
 
-        folded_b = fold("folded_b", pair_b.rearrange("p k i -> p (k i)"))
+        grouped_t = by_group(pair_t.rearrange("p k i -> p (k i)"))
+        folded_t = sb("folded_t", [P, 2 * GROUPS, PER_GROUP // 2])
+        nc.gpsimd.tensor_tensor(
+            out=folded_t[:],
+            in0=grouped_t[:, :, 0 : PER_GROUP // 2],
+            in1=grouped_t[:, :, PER_GROUP // 2 : PER_GROUP],
+            op=add,
+        )
         group_sum(sums_c[:, 0, :], by_group(pair_c[:, 0, :]))
+        group_sum(sums_t[:], folded_t[:])
+        nc.vector.reciprocal(out=r2, in_=sums_p[:, GROUPS : 2 * GROUPS])
+        nc.scalar.activation(out=neg_s1, in_=sums_p[:, 0:GROUPS], func=ACT.Copy, scale=-1.0)
         group_sum(sums_c[:, 1, :], by_group(pair_c[:, 1, :]))
-        group_sum(sums_b[:], folded_b[:])
-        nc.vector.scalar_tensor_tensor(out=neg_c, in0=neg_s1, scalar=rho2, in1=r2, op0=mult, op1=mult)
-        nc.vector.tensor_tensor(out=tau, in0=sums_b[:, G : 2 * G], in1=r2, op=mult)
+
+        nc.vector.scalar_tensor_tensor(out=neg_kc, in0=neg_s1, scalar=rho2, in1=r2, op0=mult, op1=mult)
+        nc.vector.tensor_tensor(out=tau, in0=sums_t[:, GROUPS : 2 * GROUPS], in1=r2, op=mult)
         nc.vector.tensor_tensor(out=means[:], in0=sums_c[:], in1=both(r2), op=mult)
-        add_term("terms_ct", pair_c[:, 1, :], neg_c)
-        nc.vector.scalar_tensor_tensor(out=shift[:], in0=tau, scalar=neg_t, in1=neg_s1, op0=sub, op1=mult)
+        add_term("terms_ct", pair_c[:, 1, :], neg_kc)
+        nc.vector.scalar_tensor_tensor(out=shift[:], in0=tau, scalar=neg_tbar, in1=neg_s1, op0=sub, op1=mult)
         nc.vector.scalar_tensor_tensor(
-            out=scratch[:, 0, :], in0=sums_c[:, 0, :], scalar=neg_half_rz, in1=neg_c, op0=mult, op1=mult, accum_out=read[:]
+            out=summands[:, 0, :],
+            in0=sums_c[:, 0, :],
+            scalar=neg_half_rz,
+            in1=neg_kc,
+            op0=mult,
+            op1=mult,
+            accum_out=rho_f[:],
         )
-        nc.vector.tensor_tensor(out=w, in0=sums_b[:, 0:G], in1=shift[:], op=add)
-        nc.vector.tensor_tensor(out=b_mtau[:, 1:3, :], in0=neg_c_tau, in1=both(m), op=mult)
-        nc.vector.scalar_tensor_tensor(out=e, in0=w, scalar=rho2, in1=r2, op0=mult, op1=mult)
-        nc.vector.tensor_scalar(out=coef_b[:, 0, :], in0=m, scalar1=rho, scalar2=read[:], op0=mult, op1=sub)
+        nc.vector.tensor_tensor(out=w, in0=sums_t[:, 0:GROUPS], in1=shift[:], op=add)
+        nc.vector.tensor_tensor(out=t_mtau[:, 1:3, :], in0=neg_kc_tau, in1=both(m), op=mult)
+        nc.vector.scalar_tensor_tensor(out=ke, in0=w, scalar=rho2, in1=r2, op0=mult, op1=mult)
+        nc.vector.tensor_scalar(out=coef_t[:, 0, :], in0=m, scalar1=rho, scalar2=rho_f[:], op0=mult, op1=sub)
         nc.vector.scalar_tensor_tensor(
-            out=scratch[:, 1:3, :], in0=w_s1[:], scalar=neg_rz, in1=means[:], op0=mult, op1=mult, accum_out=neg_dread[:]
+            out=summands[:, 1:3, :], in0=w_s1[:], scalar=neg_rz, in1=means[:], op0=mult, op1=mult, accum_out=neg_df[:]
         )
-        add_term("terms_cc", pair_c[:, 0, :], e)
+        add_term("terms_cc", pair_c[:, 0, :], ke)
         nc.vector.tensor_tensor(out=neg_dm, in0=neg_dm, in1=mtau, op=add)
 
         back_ps = []
         for half in range(2):
-            terms = pair_terms("terms_b", pair_b, coef_b, half)
-            blocks = (2 * half, 2 * half + 1)
-            for k in range(2):
-                add_blocks(terms[:, k].rearrange("p g j -> p (g j)"), blocks, False, k == 1)
-            total = sb("total%d" % half, [P, 2, P])
+            terms_t = pair_terms("terms_t", pair_t, coef_t, half)
+            flat = terms_t[:].rearrange("p k g j -> p k (g j)")
+            blocks = range(half * BLOCKS // 2, (half + 1) * BLOCKS // 2)
+            for n, block in enumerate(blocks):
+                for k in range(2):
+                    turn(total_ps[block][:, 0:P], flat[:, k, n * P : (n + 1) * P], False, k == 1)
+            total = sb("total%d" % half, [P, BLOCKS // 2, P])
             back_ps.append(bank(1 + half, "back_ps%d" % half))
             for n, block in enumerate(blocks):
                 nc.scalar.copy(out=total[:, n, :], in_=total_ps[block][:, 0:P])
                 turn(back_ps[half][:, n * P : (n + 1) * P], total[:, n, :], True, True)
 
-        ec = sb("ec", [P, 2, G])
-        nc.vector.tensor_tensor(out=ec[:], in0=coef_c, in1=means[:], op=mult)
-        v = sb("v", [P, G])
-        nc.vector.tensor_scalar(out=v[:], in0=neg_dm, scalar1=neg_dread[:], scalar2=neg_rho, op0=sub, op1=mult)
-        coef_a = sb("coef_a", [P, 2, G])
+        ke_m_kc_dm = sb("ke_m_kc_dm", [P, 2, GROUPS])
+        nc.vector.tensor_tensor(out=ke_m_kc_dm[:], in0=coef_c, in1=means[:], op=mult)
+        rho_dm_df = sb("rho_dm_df", [P, GROUPS])
+        nc.vector.tensor_scalar(out=rho_dm_df[:], in0=neg_dm, scalar1=neg_df[:], scalar2=neg_rho, op0=sub, op1=mult)
+        coef_p = sb("coef_p", [P, 2, GROUPS])
         nc.vector.scalar_tensor_tensor(
-            out=coef_a[:, 1, :], in0=ec[:, 0, :], scalar=-1.0, in1=ec[:, 1, :], op0=mult, op1=sub
+            out=coef_p[:, 1, :], in0=ke_m_kc_dm[:, 0, :], scalar=-1.0, in1=ke_m_kc_dm[:, 1, :], op0=mult, op1=sub
         )
         nc.vector.scalar_tensor_tensor(
-            out=coef_a[:, 0, :], in0=coef_b[:, 0, :], scalar=neg_t, in1=v[:], op0=mult, op1=add
+            out=coef_p[:, 0, :], in0=coef_t[:, 0, :], scalar=neg_tbar, in1=rho_dm_df[:], op0=mult, op1=add
         )
 
-        terms_a = [pair_terms("terms_a", pair_a, coef_a, half) for half in range(2)]
-        sum_a = sb("sum_a", [P, 2, HALF, J])
-        result = sb("result", [P, 2, HALF * J])
+        terms_p = [pair_terms("terms_p", pair_p, coef_p, half) for half in range(2)]
+        sum_p = sb("sum_p", [P, 2, HALF_GROUPS, PER_GROUP])
+        result = sb("result", [P, 2, HALF_SLOTS])
         for half in range(2):
-            nc.vector.tensor_tensor(out=sum_a[:, half], in0=terms_a[half][:, 0], in1=terms_a[half][:, 1], op=add)
+            nc.vector.tensor_tensor(out=sum_p[:, half], in0=terms_p[half][:, 0], in1=terms_p[half][:, 1], op=add)
         for half in range(2):
             nc.vector.tensor_tensor(
                 out=result[:, half],
-                in0=back_ps[half][:, 0 : 2 * P],
-                in1=sum_a[:, half].rearrange("p g j -> p (g j)"),
+                in0=back_ps[half][:, 0:HALF_SLOTS],
+                in1=sum_p[:, half].rearrange("p g j -> p (g j)"),
                 op=add,
             )
-            nc.sync.dma_start(out=out[:, half * HALF * J : (half + 1) * HALF * J], in_=result[:, half])
+            nc.sync.dma_start(out=out[:, half * HALF_SLOTS : (half + 1) * HALF_SLOTS], in_=result[:, half])

from contextlib import ExitStack

import concourse.mybir as mybir
from concourse.masks import make_identity

FEATURES, TOKENS, SLOTS, ROWS, GROUPS = 512, 2048, 512, 128, 64
PER_GROUP = SLOTS // GROUPS
FLOPS = 3 * 2 * FEATURES * ROWS * SLOTS

F32 = mybir.dt.float32
BF16 = mybir.dt.bfloat16
I32 = mybir.dt.int32
U32 = mybir.dt.uint32
U16 = mybir.dt.uint16
U8 = mybir.dt.uint8
FP8X4 = mybir.dt.float8_e4m3fn_x4
FP4X4 = mybir.dt.float4_e2m1fn_x4
ALU = mybir.AluOpType
ACT = mybir.ActivationFunctionType
AX = mybir.AxisListType

P = 128
PACK = 4
QUADRANTS, SCALE_ROWS = 4, 4
SIZE_COLS = SLOTS // P
BLOCKS = SLOTS // P
HALF_SLOTS, HALF_GROUPS = SLOTS // 2, GROUPS // 2
OUT_SCALE = 512.0
SUM_FLOOR = 1e-30
ROW_FACTORS = (OUT_SCALE, 2 * OUT_SCALE, -OUT_SCALE, -1.0, -0.5)


def tile_attend_hvshareofshare_kernel(
    tc, query, keys_words, keys_scales, gout, vals_words, vals_scales, size, dquery, base, offs, out
):
    nc = tc.nc
    mult, add, sub = ALU.mult, ALU.add, ALU.subtract

    with ExitStack() as ctx:
        keep = ctx.enter_context(tc.tile_pool(name="keep", bufs=1))
        psum = ctx.enter_context(tc.psum_pool(name="psum", bufs=1))

        def bank(n, name):
            return psum.tile([P, SLOTS], F32, tag="bank%d" % n, name=name)

        def sb(name, shape, dtype=F32, tag=None):
            return keep.tile(shape, dtype, name=name, tag=tag or name, align_bytes=64)

        offsets = keep.tile([P, SLOTS // 16], U16, name="offsets")
        k_bytes = sb("k_bytes", [P, TOKENS], U8)
        v_bytes = sb("v_bytes", [P, TOKENS], U8)
        k_words = sb("k_words", [P, TOKENS], U16)
        v_words = sb("v_words", [P, TOKENS], U16)
        zero = sb("zero", [P, 1], tag="zero_then_places")
        one = sb("one", [P, 1])
        ident = sb("ident", [P, P])
        factors = sb("factors", [P, len(ROW_FACTORS)])
        size_col = sb("size_col", [P, SIZE_COLS], tag="size_then_q_codes")
        q_raw = sb("q_raw", [P, PACK, ROWS], tag="q_then_base")
        dq_g_raw = sb("dq_g_raw", [P, 2, PACK, ROWS], tag="rows_then_p")

        nc.vector.memset(k_bytes[:].bitcast(I32), 0)
        nc.vector.memset(zero[:], 0.0)
        nc.vector.memset(v_bytes[:].bitcast(I32), 0)
        make_identity(nc, ident[:])
        for col, factor in enumerate(ROW_FACTORS):
            nc.gpsimd.memset(factors[:, col : col + 1], factor)

        def load_scales(tile, scales):
            for quad in range(QUADRANTS):
                nc.sync.dma_start(
                    out=tile[32 * quad : 32 * quad + SCALE_ROWS, :].bitcast(I32),
                    in_=scales[0, SCALE_ROWS * quad : SCALE_ROWS * (quad + 1), :].bitcast(I32),
                )

        def load_rows(raw, source):
            nc.sync.dma_start(out=raw, in_=source.rearrange("(p r) w -> p r w", r=PACK))

        nc.sync.dma_start(offsets[:], offs)
        nc.sync.dma_start(out=k_words[:].bitcast(I32), in_=keys_words[0].bitcast(I32))
        nc.sync.dma_start(out=size_col[:], in_=size.rearrange("o (p r) -> (o p) r", r=SIZE_COLS))
        load_rows(q_raw[:], query)
        load_scales(k_bytes, keys_scales)
        nc.sync.dma_start(out=v_words[:].bitcast(I32), in_=vals_words[0].bitcast(I32))
        load_rows(dq_g_raw[:, 0], dquery)
        load_rows(dq_g_raw[:, 1], gout)
        load_scales(v_bytes, vals_scales)

        nc.scalar.activation(out=one[:], in_=zero[:], func=ACT.Exp)

        def interleave(grouped, raw):
            nc.scalar.copy(out=grouped, in_=raw.rearrange("p r w -> p w r"))

        def quantize(name, grouped, tag):
            width = grouped.shape[1]
            codes = sb(name + "_codes", [P, width], U32, tag=tag)
            scales = sb(name + "_scales", [P, width], U8)
            nc.vector.quantize_mx(
                out=codes[:].bitcast(FP8X4), scales=scales[:], in_=grouped[:].rearrange("p w r -> p (w r)")
            )
            return codes, scales

        def gather(name, window, dtype, tag=None):
            picked = sb(name, [P, SLOTS], dtype, tag=tag)
            nc.vector.tensor_copy(picked[:], window[:].indirect(offsets[:]))
            return picked

        def scores(acc, quantized, first, words, scale_bytes):
            codes, scales = quantized
            nc.tensor.matmul_mx(
                out=acc[:],
                lhsT=codes[:, first : first + ROWS].bitcast(FP8X4),
                lhsT_scale=scales[:, first : first + ROWS],
                rhs=words[:].bitcast(FP4X4),
                rhs_scale=scale_bytes[:],
                start=True,
                stop=True,
            )

        def turn(acc, block, start, stop):
            nc.tensor.matmul(out=acc, lhsT=block, rhs=ident[:], is_transpose=True, start=start, stop=stop)

        q_bf = sb("q_bf", [P, ROWS, PACK], BF16, tag="q_bf_then_v_picked")
        interleave(q_bf[:], q_raw[:])
        base_sb = sb("base_sb", [P, SLOTS], tag="q_then_base")
        nc.sync.dma_start(out=base_sb[:], in_=base)

        size_ps = bank(3, "size_ps")
        for r in range(SIZE_COLS):
            turn(size_ps[:, r * P : (r + 1) * P], size_col[:, r : r + 1].to_broadcast([P, P]), True, True)
        size_row = sb("size_row", [P, SLOTS])
        nc.scalar.activation(
            out=size_row[:].rearrange("p (s r) -> p s r", r=SIZE_COLS),
            in_=size_ps[:].rearrange("p (r s) -> p s r", r=SIZE_COLS),
            func=ACT.Copy,
            scale=one[:],
        )
        dq_g_bf = sb("dq_g_bf", [P, 2 * ROWS, PACK], BF16)
        interleave(dq_g_bf[:, 0:ROWS, :], dq_g_raw[:, 0])
        interleave(dq_g_bf[:, ROWS : 2 * ROWS, :], dq_g_raw[:, 1])

        k_words_picked = gather("k_words_picked", k_words, U16)
        k_bytes_picked = gather("k_bytes_picked", k_bytes, U8)
        q_mx = quantize("q", q_bf, "size_then_q_codes")
        a_ps = bank(0, "a_ps")
        scores(a_ps, q_mx, 0, k_words_picked, k_bytes_picked)
        v_words_picked = gather("v_words_picked", v_words, U16, tag="q_bf_then_v_picked")
        neg_max = sb("neg_max", [P, 1])
        nc.vector.tensor_reduce(out=neg_max[:], in_=a_ps[:], axis=AX.X, op=ALU.max, negate=True)
        dq_g_mx = quantize("dq_g", dq_g_bf, "v_words")
        t_ps = bank(1, "t_ps")
        scores(t_ps, dq_g_mx, 0, k_words_picked, k_bytes_picked)
        v_bytes_picked = gather("v_bytes_picked", v_bytes, U8)
        c_ps = bank(2, "c_ps")
        scores(c_ps, dq_g_mx, ROWS, v_words_picked, v_bytes_picked)

        pair_p = sb("pair_p", [P, 2, SLOTS], tag="rows_then_p")
        t_and_rz = sb("t_and_rz", [P, 2 * SLOTS + 1], tag="v_bytes")
        pair_t = t_and_rz[:, 0 : 2 * SLOTS].rearrange("p (k i) -> p k i", k=2)
        rz = t_and_rz[:, 2 * SLOTS : 2 * SLOTS + 1]
        pair_c = sb("pair_c", [P, 2, SLOTS])
        p, p2 = pair_p[:, 0, :], pair_p[:, 1, :]
        p2_size = sb("p2_size", [P, SLOTS], tag="p2_size_then_coefs")
        z = sb("z", [P, 1])
        nc.scalar.activation(out=p, in_=a_ps[:], func=ACT.Exp, bias=neg_max[:], accum_out=z[:])
        nc.scalar.activation(out=p2, in_=p, func=ACT.Square, bias=zero[:])
        nc.gpsimd.tensor_tensor(out=p2_size[:], in0=p2, in1=size_row[:], op=mult)

        xz = sb("xz", [P, 1])
        nc.vector.reciprocal(out=rz, in_=z[:])
        nc.vector.scalar_tensor_tensor(
            out=pair_t[:, 0, :], in0=t_ps[:], scalar=1.0, in1=p, op0=mult, op1=mult, accum_out=xz[:]
        )
        nc.vector.scalar_tensor_tensor(out=pair_t[:, 1, :], in0=t_ps[:], scalar=2.0, in1=p2, op0=mult, op1=mult)
        nc.vector.tensor_tensor(out=pair_c[:, 0, :], in0=c_ps[:], in1=p2_size[:], op=mult)
        nc.vector.scalar_tensor_tensor(
            out=pair_c[:, 1, :], in0=t_ps[:], scalar=-2.0, in1=pair_c[:, 0, :], op0=mult, op1=mult
        )

        places = sb("places", [P, PER_GROUP, 2, GROUPS], tag="zero_then_places")
        nc.scalar.activation(
            out=places[:, :, 0, :],
            in_=a_ps[:].rearrange("p (g j) -> p j g", j=PER_GROUP),
            func=ACT.Exp,
            bias=neg_max[:],
        )
        nc.scalar.activation(out=places[:, :, 1, :], in_=places[:, :, 0, :], func=ACT.Square)
        row_scalars = sb("row_scalars", [P, len(ROW_FACTORS) + 1])
        rho, rho2, neg_rho, neg_rz, neg_half_rz, neg_tbar = [
            row_scalars[:, col : col + 1] for col in range(len(ROW_FACTORS) + 1)
        ]
        nc.scalar.activation(out=row_scalars[:, 0 : len(ROW_FACTORS)], in_=factors[:], func=ACT.Copy, scale=rz)
        nc.scalar.activation(out=neg_tbar, in_=xz[:], func=ACT.Copy, scale=neg_rz)
        turned_ps = bank(3, "turned_ps")
        for j in range(PER_GROUP):
            turn(turned_ps[:, 0:P], places[:, j, :, :].rearrange("p k g -> p (k g)"), j == 0, j == PER_GROUP - 1)
        turned = sb("turned", [P, P])
        nc.scalar.activation(out=turned[:], in_=turned_ps[:, 0:P], func=ACT.Copy, bias=SUM_FLOOR)
        sums_p = bank(4, "sums_p")
        turn(sums_p[:, 0:P], turned[:], True, True)

        total_ps = [bank(n, "total_ps%d" % n) for n in (5, 6, 7, 0)]

        def add_blocks(terms, start):
            for block in range(BLOCKS):
                turn(total_ps[block][:, 0:P], terms[:, block * P : (block + 1) * P], start, False)

        def by_group(ap):
            return ap.rearrange("p (g j) -> p g j", j=PER_GROUP)

        def group_sum(sums, values):
            nc.vector.tensor_reduce(out=sums, in_=values, axis=AX.X, op=add)

        def spread(coef):
            return coef.unsqueeze(len(coef.shape)).to_broadcast(list(coef.shape) + [PER_GROUP])

        def both(ap):
            return ap.unsqueeze(1).to_broadcast([P, 2, GROUPS])

        def add_term(name, values, coef):
            terms = sb(name, [P, SLOTS])
            nc.vector.tensor_tensor(out=by_group(terms[:]), in0=by_group(values), in1=spread(coef), op=mult)
            add_blocks(terms[:], False)

        def pair_terms(name, pair, coef, half):
            terms = sb("%s%d" % (name, half), [P, 2, HALF_GROUPS, PER_GROUP])
            nc.vector.tensor_tensor(
                out=terms[:],
                in0=pair[:, :, half * HALF_SLOTS : (half + 1) * HALF_SLOTS].rearrange(
                    "p k (g j) -> p k g j", j=PER_GROUP
                ),
                in1=spread(coef[:, :, half * HALF_GROUPS : (half + 1) * HALF_GROUPS]),
                op=mult,
            )
            return terms

        add_blocks(base_sb[:], True)

        sums_t = sb("sums_t", [P, 2 * GROUPS])
        sums_c = sb("sums_c", [P, 2, GROUPS])
        coefs = sb("coefs", [P, 4, GROUPS], tag="p2_size_then_coefs")
        coef_c, neg_kc_tau = coefs[:, 0:2, :], coefs[:, 1:3, :]
        ke, neg_kc, tau, r2 = coefs[:, 0, :], coefs[:, 1, :], coefs[:, 2, :], coefs[:, 3, :]
        w_s1 = sb("w_s1", [P, 2, GROUPS])
        w, neg_s1 = w_s1[:, 0, :], w_s1[:, 1, :]
        means = sb("means", [P, 2, GROUPS])
        m, neg_dm = means[:, 0, :], means[:, 1, :]
        shift = sb("shift", [P, GROUPS])
        summands = sb("summands", [P, 3, GROUPS])
        rho_f = sb("rho_f", [P, 1])
        neg_df = sb("neg_df", [P, 1])
        t_mtau = sb("t_mtau", [P, 3, GROUPS])
        coef_t, mtau = t_mtau[:, 0:2, :], t_mtau[:, 2, :]

        grouped_t = by_group(pair_t.rearrange("p k i -> p (k i)"))
        folded_t = sb("folded_t", [P, 2 * GROUPS, PER_GROUP // 2])
        nc.gpsimd.tensor_tensor(
            out=folded_t[:],
            in0=grouped_t[:, :, 0 : PER_GROUP // 2],
            in1=grouped_t[:, :, PER_GROUP // 2 : PER_GROUP],
            op=add,
        )
        group_sum(sums_c[:, 0, :], by_group(pair_c[:, 0, :]))
        group_sum(sums_t[:], folded_t[:])
        nc.vector.reciprocal(out=r2, in_=sums_p[:, GROUPS : 2 * GROUPS])
        nc.scalar.activation(out=neg_s1, in_=sums_p[:, 0:GROUPS], func=ACT.Copy, scale=-1.0)
        group_sum(sums_c[:, 1, :], by_group(pair_c[:, 1, :]))

        nc.vector.scalar_tensor_tensor(out=neg_kc, in0=neg_s1, scalar=rho2, in1=r2, op0=mult, op1=mult)
        nc.vector.tensor_tensor(out=tau, in0=sums_t[:, GROUPS : 2 * GROUPS], in1=r2, op=mult)
        nc.vector.tensor_tensor(out=means[:], in0=sums_c[:], in1=both(r2), op=mult)
        add_term("terms_ct", pair_c[:, 1, :], neg_kc)
        nc.vector.scalar_tensor_tensor(out=shift[:], in0=tau, scalar=neg_tbar, in1=neg_s1, op0=sub, op1=mult)
        nc.vector.scalar_tensor_tensor(
            out=summands[:, 0, :],
            in0=sums_c[:, 0, :],
            scalar=neg_half_rz,
            in1=neg_kc,
            op0=mult,
            op1=mult,
            accum_out=rho_f[:],
        )
        nc.vector.tensor_tensor(out=w, in0=sums_t[:, 0:GROUPS], in1=shift[:], op=add)
        nc.vector.tensor_tensor(out=t_mtau[:, 1:3, :], in0=neg_kc_tau, in1=both(m), op=mult)
        nc.vector.scalar_tensor_tensor(out=ke, in0=w, scalar=rho2, in1=r2, op0=mult, op1=mult)
        nc.vector.tensor_scalar(out=coef_t[:, 0, :], in0=m, scalar1=rho, scalar2=rho_f[:], op0=mult, op1=sub)
        nc.vector.scalar_tensor_tensor(
            out=summands[:, 1:3, :], in0=w_s1[:], scalar=neg_rz, in1=means[:], op0=mult, op1=mult, accum_out=neg_df[:]
        )
        add_term("terms_cc", pair_c[:, 0, :], ke)
        nc.vector.tensor_tensor(out=neg_dm, in0=neg_dm, in1=mtau, op=add)

        back_ps = []
        for half in range(2):
            terms_t = pair_terms("terms_t", pair_t, coef_t, half)
            flat = terms_t[:].rearrange("p k g j -> p k (g j)")
            blocks = range(half * BLOCKS // 2, (half + 1) * BLOCKS // 2)
            for n, block in enumerate(blocks):
                for k in range(2):
                    turn(total_ps[block][:, 0:P], flat[:, k, n * P : (n + 1) * P], False, k == 1)
            total = sb("total%d" % half, [P, BLOCKS // 2, P])
            back_ps.append(bank(1 + half, "back_ps%d" % half))
            for n, block in enumerate(blocks):
                nc.scalar.copy(out=total[:, n, :], in_=total_ps[block][:, 0:P])
                turn(back_ps[half][:, n * P : (n + 1) * P], total[:, n, :], True, True)

        ke_m_kc_dm = sb("ke_m_kc_dm", [P, 2, GROUPS])
        nc.vector.tensor_tensor(out=ke_m_kc_dm[:], in0=coef_c, in1=means[:], op=mult)
        rho_dm_df = sb("rho_dm_df", [P, GROUPS])
        nc.vector.tensor_scalar(out=rho_dm_df[:], in0=neg_dm, scalar1=neg_df[:], scalar2=neg_rho, op0=sub, op1=mult)
        coef_p = sb("coef_p", [P, 2, GROUPS])
        nc.vector.scalar_tensor_tensor(
            out=coef_p[:, 1, :], in0=ke_m_kc_dm[:, 0, :], scalar=-1.0, in1=ke_m_kc_dm[:, 1, :], op0=mult, op1=sub
        )
        nc.vector.scalar_tensor_tensor(
            out=coef_p[:, 0, :], in0=coef_t[:, 0, :], scalar=neg_tbar, in1=rho_dm_df[:], op0=mult, op1=add
        )

        terms_p = [pair_terms("terms_p", pair_p, coef_p, half) for half in range(2)]
        sum_p = sb("sum_p", [P, 2, HALF_GROUPS, PER_GROUP])
        result = sb("result", [P, 2, HALF_SLOTS])
        for half in range(2):
            nc.vector.tensor_tensor(out=sum_p[:, half], in0=terms_p[half][:, 0], in1=terms_p[half][:, 1], op=add)
        for half in range(2):
            nc.vector.tensor_tensor(
                out=result[:, half],
                in0=back_ps[half][:, 0:HALF_SLOTS],
                in1=sum_p[:, half].rearrange("p g j -> p (g j)"),
                op=add,
            )
            nc.sync.dma_start(out=out[:, half * HALF_SLOTS : (half + 1) * HALF_SLOTS], in_=result[:, half])
